import numpy as np
import ml_dtypes


def mxq(x, axis, fmt="e4m3"):
    dtype, down = {"e4m3": (ml_dtypes.float8_e4m3fn, 7), "e5m2": (ml_dtypes.float8_e5m2, 14)}[fmt]
    v = np.moveaxis(np.asarray(x, np.float32).astype(ml_dtypes.bfloat16).astype(np.float64), axis, -1)
    blocks = v.reshape(v.shape[:-1] + (-1, 32))
    amax = np.abs(blocks).max(-1, keepdims=True)
    byte = np.maximum(np.where(amax > 0, np.frexp(amax)[1] - 1 + 127, 0) - down, 1)
    scale = np.exp2(byte - 127.0)
    codes = (blocks / scale).astype(np.float32).astype(dtype).astype(np.float64)
    return np.moveaxis((codes * scale).reshape(v.shape), -1, axis)


WIDE = False


def mx_kscale(k):
    if not WIDE:
        return np.ones(k)
    levels = np.array([18, -18])
    if k % 512:
        return np.exp2(np.random.permutation(np.resize(levels, k // 32))).repeat(32)
    a = np.empty((k // 512, 16))
    for p in range(k // 512):
        a[p, :8] = np.random.permutation(np.resize(levels, 8))
        for g in range(8):
            far = levels[np.abs(levels - a[p, g]) >= 10]
            a[p, g + 8] = far[np.random.randint(len(far))]
    return np.exp2(a.ravel()).repeat(32)


def f64(x):
    return np.asarray(x).astype(np.float64)


def striped(idx):
    return np.tile(np.asarray(idx).reshape(-1, 16).T, (8, 1)).astype(np.uint16)


def unstriped(offs):
    return offs[:16].T.reshape(-1).astype(np.int64)


B, N, T, D, DV, NQ = 1, 512, 2048, 512, 512, 128


def setup_inputs():
    n = np.random.standard_normal
    idx = np.random.permutation(T)[:B * N]
    u = mx_kscale(B * N)
    ut = np.ones(T)
    ut[idx] = u
    w = np.exp(n((B, N, NQ)))
    w = w / w.sum(1, keepdims=True)
    return {
        "wT": (w * u.reshape(B, N, 1)).astype(np.float32),
        "vT": (n((DV, T)) / ut).astype(np.float32),
        "offs": striped(idx),
    }


def reference(wT, vT, offs):
    idx = unstriped(offs)
    pick = lambda x: x[:, idx].reshape(x.shape[0], B, N).transpose(1, 0, 2)
    return mxq(f64(wT), 1, "e5m2").transpose(0, 2, 1) @ mxq(pick(f64(vT)).transpose(0, 2, 1), 1, "e4m3")

@@ -1,0 +1,108 @@
+from contextlib import ExitStack
+
+import concourse.mybir as mybir
+from concourse.masks import make_identity
+
+N, T, DV, NQ = 512, 2048, 512, 128
+FLOPS = 2 * N * NQ * DV
+
+P = 128
+PACK = 4
+BLOCKS = DV // P
+
+F32 = mybir.dt.float32
+BF16 = mybir.dt.bfloat16
+U32 = mybir.dt.uint32
+U16 = mybir.dt.uint16
+U8 = mybir.dt.uint8
+E4M3X4 = mybir.dt.float8_e4m3fn_x4
+E5M2X4 = mybir.dt.float8_e5m2_x4
+
+
+def tile_attend_spmm_kernel(tc, wT, vT, offs, out):
+    nc = tc.nc
+    with ExitStack() as ctx:
+        hold = ctx.enter_context(tc.tile_pool(name="hold", bufs=1))
+        psum = ctx.enter_context(tc.psum_pool(name="psum", bufs=1))
+
+        ident = hold.tile([P, P], F32, name="ident")
+        make_identity(nc, ident[:])
+
+        offsets = hold.tile([P, N // 16], U16, name="offsets")
+        pool_v = [hold.tile([P, T], F32, name=f"pool_v{b}", tag=f"pool{b}", align_bytes=64) for b in range(BLOCKS)]
+        w_raw = hold.tile([P, PACK, NQ], F32, name="w_raw", align_bytes=64)
+
+        for b in range(BLOCKS):
+            nc.sync.dma_start(out=pool_v[b][:], in_=vT[b * P:(b + 1) * P, :])
+            if b == 0:
+                nc.sync.dma_start(offsets[:], offs)
+        nc.sync.dma_start(out=w_raw[:], in_=wT.flatten_outer_dims().rearrange("(p t) q -> p t q", t=PACK))
+
+        v_codes = hold.tile([P, DV], U32, name="v_codes", align_bytes=64)
+        v_scales = hold.tile([P, DV], U8, name="v_scales", align_bytes=64)
+        w_codes = hold.tile([P, NQ], U32, name="w_codes", align_bytes=64)
+        w_scales = hold.tile([P, NQ], U8, name="w_scales", align_bytes=64)
+
+        turned = {}
+        grouped = {}
+
+        def gather(b):
+            picked = hold.tile([P, 2, P, 2], BF16, name=f"picked{b}", align_bytes=64)
+            nc.vector.tensor_copy(picked[:].rearrange("d u p e -> d p u e"), pool_v[b][:].indirect(offsets[:]))
+            words = picked[:].rearrange("d u p e -> d (u p e)").bitcast(F32)
+            turned[b] = psum.tile([P, 2, P], F32, name=f"turned{b}")
+            for u in range(2):
+                nc.tensor.transpose(turned[b][:, u, :], words[:, u * P:(u + 1) * P], ident[:])
+
+        def group(b):
+            g = hold.tile([P, P, PACK], BF16, name=f"grouped{b}", tag=f"pool{b + 1}", align_bytes=64)
+            nc.scalar.copy(out=g[:].bitcast(F32), in_=turned[b][:].rearrange("p u r -> p r u"))
+            grouped[b] = g
+
+        def quantize(b):
+            cols = slice(b * P, (b + 1) * P)
+            nc.vector.quantize_mx(
+                out=v_codes[:, cols].bitcast(E4M3X4),
+                scales=v_scales[:, cols],
+                in_=grouped[b][:].rearrange("p r t -> p (r t)"),
+            )
+
+        gather(0)
+        for b in range(1, BLOCKS - 1):
+            gather(b)
+            group(b - 1)
+            quantize(b - 1)
+        gather(BLOCKS - 1)
+        w_grouped = hold.tile([P, NQ, PACK], BF16, name="w_grouped", align_bytes=64)
+        middle = NQ // 2
+        by_query = w_raw[:].rearrange("p t q -> p q t")
+        nc.scalar.copy(out=w_grouped[:, :middle], in_=by_query[:, :middle])
+        nc.vector.tensor_copy(out=w_grouped[:, middle:], in_=by_query[:, middle:])
+        group(BLOCKS - 2)
+        quantize(BLOCKS - 2)
+        nc.vector.quantize_mx(
+            out=w_codes[:].bitcast(E5M2X4),
+            scales=w_scales[:],
+            in_=w_grouped[:].rearrange("p q t -> p (q t)"),
+        )
+        group(BLOCKS - 1)
+        quantize(BLOCKS - 1)
+
+        acc = psum.tile([NQ, DV], F32, name="acc")
+        nc.tensor.matmul_mx(
+            out=acc[:],
+            lhsT=w_codes[:].bitcast(E5M2X4),
+            lhsT_scale=w_scales[:],
+            rhs=v_codes[:].bitcast(E4M3X4),
+            rhs_scale=v_scales[:],
+            start=True,
+            stop=True,
+        )
+        result = out.flatten_outer_dims()
+        half = DV // 2
+        left = hold.tile([NQ, half], F32, name="left")
+        right = hold.tile([NQ, half], F32, name="right")
+        nc.vector.tensor_copy(left[:], acc[:, 0:half])
+        nc.sync.dma_start(out=result[:, 0:half], in_=left[:])
+        nc.scalar.copy(out=right[:], in_=acc[:, half:DV])
+        nc.scalar.dma_start(out=result[:, half:DV], in_=right[:])

@@ -25,8 +25,10 @@ def tile_attend_spmm_kernel(tc, wT, vT, offs, out):
         hold = ctx.enter_context(tc.tile_pool(name="hold", bufs=1))
         psum = ctx.enter_context(tc.psum_pool(name="psum", bufs=1))
 
+        ident_made = hold.tile([P, P], F32, name="ident_made")
+        make_identity(nc, ident_made[:])
         ident = hold.tile([P, P], F32, name="ident")
-        make_identity(nc, ident[:])
+        nc.scalar.copy(out=ident[:], in_=ident_made[:])
 
         offsets = hold.tile([P, N // 16], U16, name="offsets")
         pool_v = [hold.tile([P, T], F32, name=f"pool_v{b}", tag=f"pool{b}", align_bytes=64) for b in range(BLOCKS)]
@@ -99,10 +101,10 @@ def tile_attend_spmm_kernel(tc, wT, vT, offs, out):
             stop=True,
         )
         result = out.flatten_outer_dims()
-        half = DV // 2
-        left = hold.tile([NQ, half], F32, name="left")
-        right = hold.tile([NQ, half], F32, name="right")
-        nc.vector.tensor_copy(left[:], acc[:, 0:half])
-        nc.sync.dma_start(out=result[:, 0:half], in_=left[:])
-        nc.scalar.copy(out=right[:], in_=acc[:, half:DV])
-        nc.scalar.dma_start(out=result[:, half:DV], in_=right[:])
+        piece = DV // 4
+        for h in range(4):
+            cols = slice(h * piece, (h + 1) * piece)
+            staged = hold.tile([NQ, piece], F32, name=f"staged{h}")
+            nc.vector.tensor_copy(staged[:], acc[:, cols])
+            queue = nc.sync if h % 2 == 0 else nc.scalar
+            queue.dma_start(out=result[:, cols], in_=staged[:])

@@ -40,13 +40,12 @@ def tile_attend_spmm_kernel(tc, wT, vT, offs, out):
                 nc.sync.dma_start(offsets[:], offs)
         nc.sync.dma_start(out=w_raw[:], in_=wT.flatten_outer_dims().rearrange("(p t) q -> p t q", t=PACK))
 
-        v_codes = hold.tile([P, DV], U32, name="v_codes", align_bytes=64)
+        v_codes = hold.tile([P, DV], U32, name="v_codes", tag=f"pool{BLOCKS - 1}", align_bytes=64)
         v_scales = hold.tile([P, DV], U8, name="v_scales", align_bytes=64)
         w_codes = hold.tile([P, NQ], U32, name="w_codes", align_bytes=64)
         w_scales = hold.tile([P, NQ], U8, name="w_scales", align_bytes=64)
 
         turned = {}
-        grouped = {}
 
         def gather(b):
             picked = hold.tile([P, 2, P, 2], BF16, name=f"picked{b}", align_bytes=64)
@@ -56,39 +55,43 @@ def tile_attend_spmm_kernel(tc, wT, vT, offs, out):
             for u in range(2):
                 nc.tensor.transpose(turned[b][:, u, :], words[:, u * P:(u + 1) * P], ident[:])
 
-        def group(b):
-            g = hold.tile([P, P, PACK], BF16, name=f"grouped{b}", tag=f"pool{b + 1}", align_bytes=64)
-            nc.scalar.copy(out=g[:].bitcast(F32), in_=turned[b][:].rearrange("p u r -> p r u"))
-            grouped[b] = g
+        early = hold.tile([P, 2 * P, PACK], BF16, name="grouped01", align_bytes=64)
+        grouped = [early[:, :P], early[:, P:]]
+        grouped.append(hold.tile([P, P, PACK], BF16, name="grouped2", align_bytes=64)[:])
+        half = P // 2
+        last_halves = [hold.tile([P, half, PACK], BF16, name=f"grouped3_{h}", align_bytes=64) for h in range(2)]
 
-        def quantize(b):
-            cols = slice(b * P, (b + 1) * P)
+        def group(b):
+            nc.scalar.copy(out=grouped[b].bitcast(F32), in_=turned[b][:].rearrange("p u r -> p r u"))
+
+        def quantize(first, last, source):
+            cols = slice(first, last)
             nc.vector.quantize_mx(
                 out=v_codes[:, cols].bitcast(E4M3X4),
                 scales=v_scales[:, cols],
-                in_=grouped[b][:].rearrange("p r t -> p (r t)"),
+                in_=source.rearrange("p r t -> p (r t)"),
             )
 
-        gather(0)
-        for b in range(1, BLOCKS - 1):
+        for b in range(BLOCKS - 1):
             gather(b)
-            group(b - 1)
-            quantize(b - 1)
+            group(b)
         gather(BLOCKS - 1)
         w_grouped = hold.tile([P, NQ, PACK], BF16, name="w_grouped", align_bytes=64)
-        middle = NQ // 2
-        by_query = w_raw[:].rearrange("p t q -> p q t")
-        nc.scalar.copy(out=w_grouped[:, :middle], in_=by_query[:, :middle])
-        nc.vector.tensor_copy(out=w_grouped[:, middle:], in_=by_query[:, middle:])
-        group(BLOCKS - 2)
-        quantize(BLOCKS - 2)
+        nc.scalar.copy(out=w_grouped[:], in_=w_raw[:].rearrange("p t q -> p q t"))
+        for h in range(2):
+            nc.scalar.copy(
+                out=last_halves[h][:].bitcast(F32),
+                in_=turned[BLOCKS - 1][:, :, h * half:(h + 1) * half].rearrange("p u r -> p r u"),
+            )
+        quantize(0, 2 * P, early[:])
+        quantize(2 * P, 3 * P, grouped[2])
         nc.vector.quantize_mx(
             out=w_codes[:].bitcast(E5M2X4),
             scales=w_scales[:],
             in_=w_grouped[:].rearrange("p q t -> p (q t)"),
         )
-        group(BLOCKS - 1)
-        quantize(BLOCKS - 1)
+        for h in range(2):
+            quantize(3 * P + h * half, 3 * P + (h + 1) * half, last_halves[h][:])
 
         acc = psum.tile([NQ, DV], F32, name="acc")
         nc.tensor.matmul_mx(

@@ -40,7 +40,7 @@ def tile_attend_spmm_kernel(tc, wT, vT, offs, out):
                 nc.sync.dma_start(offsets[:], offs)
         nc.sync.dma_start(out=w_raw[:], in_=wT.flatten_outer_dims().rearrange("(p t) q -> p t q", t=PACK))
 
-        v_codes = hold.tile([P, DV], U32, name="v_codes", tag=f"pool{BLOCKS - 1}", align_bytes=64)
+        v_codes = hold.tile([P, DV], U32, name="v_codes", tag=f"pool{BLOCKS - 2}", align_bytes=64)
         v_scales = hold.tile([P, DV], U8, name="v_scales", align_bytes=64)
         w_codes = hold.tile([P, NQ], U32, name="w_codes", align_bytes=64)
         w_scales = hold.tile([P, NQ], U8, name="w_scales", align_bytes=64)
@@ -57,7 +57,7 @@ def tile_attend_spmm_kernel(tc, wT, vT, offs, out):
 
         early = hold.tile([P, 2 * P, PACK], BF16, name="grouped01", align_bytes=64)
         grouped = [early[:, :P], early[:, P:]]
-        grouped.append(hold.tile([P, P, PACK], BF16, name="grouped2", align_bytes=64)[:])
+        grouped.append(hold.tile([P, P, PACK], BF16, name="grouped2", tag=f"pool{BLOCKS - 1}", align_bytes=64)[:])
         half = P // 2
         last_halves = [hold.tile([P, half, PACK], BF16, name=f"grouped3_{h}", align_bytes=64) for h in range(2)]
 
@@ -72,18 +72,20 @@ def tile_attend_spmm_kernel(tc, wT, vT, offs, out):
                 in_=source.rearrange("p r t -> p (r t)"),
             )
 
-        for b in range(BLOCKS - 1):
+        for b in range(BLOCKS - 2):
             gather(b)
             group(b)
+        gather(BLOCKS - 2)
+        quantize(0, 2 * P, early[:])
         gather(BLOCKS - 1)
         w_grouped = hold.tile([P, NQ, PACK], BF16, name="w_grouped", align_bytes=64)
-        nc.scalar.copy(out=w_grouped[:], in_=w_raw[:].rearrange("p t q -> p q t"))
+        nc.vector.tensor_copy(out=w_grouped[:], in_=w_raw[:].rearrange("p t q -> p q t"))
+        group(BLOCKS - 2)
         for h in range(2):
             nc.scalar.copy(
                 out=last_halves[h][:].bitcast(F32),
                 in_=turned[BLOCKS - 1][:, :, h * half:(h + 1) * half].rearrange("p u r -> p r u"),
             )
-        quantize(0, 2 * P, early[:])
         quantize(2 * P, 3 * P, grouped[2])
         nc.vector.quantize_mx(
             out=w_codes[:].bitcast(E5M2X4),
@@ -104,10 +106,10 @@ def tile_attend_spmm_kernel(tc, wT, vT, offs, out):
             stop=True,
         )
         result = out.flatten_outer_dims()
-        piece = DV // 4
-        for h in range(4):
-            cols = slice(h * piece, (h + 1) * piece)
-            staged = hold.tile([NQ, piece], F32, name=f"staged{h}")
+        first = 0
+        for h, width in enumerate((256, 256)):
+            cols = slice(first, first + width)
+            first = first + width
+            staged = hold.tile([NQ, width], F32, name=f"staged{h}")
             nc.vector.tensor_copy(staged[:], acc[:, cols])
-            queue = nc.sync if h % 2 == 0 else nc.scalar
-            queue.dma_start(out=result[:, cols], in_=staged[:])
+            nc.sync.dma_start(out=result[:, cols], in_=staged[:])

@@ -31,13 +31,15 @@ def tile_attend_spmm_kernel(tc, wT, vT, offs, out):
         nc.scalar.copy(out=ident[:], in_=ident_made[:])
 
         offsets = hold.tile([P, N // 16], U16, name="offsets")
-        pool_v = [hold.tile([P, T], F32, name=f"pool_v{b}", tag=f"pool{b}", align_bytes=64) for b in range(BLOCKS)]
+        pool01 = hold.tile([P, 2, T], F32, name="pool01", align_bytes=64)
+        late = [hold.tile([P, T], F32, name=f"pool_v{b}", tag=f"pool{b}", align_bytes=64) for b in range(2, BLOCKS)]
+        windows = [pool01[:, 0, :], pool01[:, 1, :], late[0][:], late[1][:]]
         w_raw = hold.tile([P, PACK, NQ], F32, name="w_raw", align_bytes=64)
 
-        for b in range(BLOCKS):
-            nc.sync.dma_start(out=pool_v[b][:], in_=vT[b * P:(b + 1) * P, :])
-            if b == 0:
-                nc.sync.dma_start(offsets[:], offs)
+        nc.sync.dma_start(out=pool01[:], in_=vT[:2 * P, :].rearrange("(b p) t -> p b t", b=2))
+        nc.sync.dma_start(offsets[:], offs)
+        for b in range(2, BLOCKS):
+            nc.sync.dma_start(out=windows[b], in_=vT[b * P:(b + 1) * P, :])
         nc.sync.dma_start(out=w_raw[:], in_=wT.flatten_outer_dims().rearrange("(p t) q -> p t q", t=PACK))
 
         v_codes = hold.tile([P, DV], U32, name="v_codes", tag=f"pool{BLOCKS - 2}", align_bytes=64)
@@ -49,15 +51,15 @@ def tile_attend_spmm_kernel(tc, wT, vT, offs, out):
 
         def gather(b):
             picked = hold.tile([P, 2, P, 2], BF16, name=f"picked{b}", align_bytes=64)
-            nc.vector.tensor_copy(picked[:].rearrange("d u p e -> d p u e"), pool_v[b][:].indirect(offsets[:]))
+            nc.vector.tensor_copy(picked[:].rearrange("d u p e -> d p u e"), windows[b].indirect(offsets[:]))
             words = picked[:].rearrange("d u p e -> d (u p e)").bitcast(F32)
             turned[b] = psum.tile([P, 2, P], F32, name=f"turned{b}")
             for u in range(2):
                 nc.tensor.transpose(turned[b][:, u, :], words[:, u * P:(u + 1) * P], ident[:])
 
-        early = hold.tile([P, 2 * P, PACK], BF16, name="grouped01", align_bytes=64)
-        grouped = [early[:, :P], early[:, P:]]
-        grouped.append(hold.tile([P, P, PACK], BF16, name="grouped2", tag=f"pool{BLOCKS - 1}", align_bytes=64)[:])
+        early = hold.tile([P, P, PACK], BF16, name="grouped0", align_bytes=64)
+        middle = hold.tile([P, 2 * P, PACK], BF16, name="grouped12", tag=f"pool{BLOCKS - 1}", align_bytes=64)
+        grouped = [early[:], middle[:, :P], middle[:, P:]]
         half = P // 2
         last_halves = [hold.tile([P, half, PACK], BF16, name=f"grouped3_{h}", align_bytes=64) for h in range(2)]
 
@@ -72,26 +74,27 @@ def tile_attend_spmm_kernel(tc, wT, vT, offs, out):
                 in_=source.rearrange("p r t -> p (r t)"),
             )
 
-        for b in range(BLOCKS - 2):
-            gather(b)
-            group(b)
-        gather(BLOCKS - 2)
-        quantize(0, 2 * P, early[:])
+        gather(0)
+        group(0)
+        gather(1)
+        gather(2)
+        quantize(0, P, early[:])
         gather(BLOCKS - 1)
         w_grouped = hold.tile([P, NQ, PACK], BF16, name="w_grouped", align_bytes=64)
         nc.vector.tensor_copy(out=w_grouped[:], in_=w_raw[:].rearrange("p t q -> p q t"))
-        group(BLOCKS - 2)
+        group(1)
+        group(2)
         for h in range(2):
             nc.scalar.copy(
                 out=last_halves[h][:].bitcast(F32),
                 in_=turned[BLOCKS - 1][:, :, h * half:(h + 1) * half].rearrange("p u r -> p r u"),
             )
-        quantize(2 * P, 3 * P, grouped[2])
         nc.vector.quantize_mx(
             out=w_codes[:].bitcast(E5M2X4),
             scales=w_scales[:],
             in_=w_grouped[:].rearrange("p q t -> p (q t)"),
         )
+        quantize(P, 3 * P, middle[:])
         for h in range(2):
             quantize(3 * P + h * half, 3 * P + (h + 1) * half, last_halves[h][:])
 
@@ -107,7 +110,7 @@ def tile_attend_spmm_kernel(tc, wT, vT, offs, out):
         )
         result = out.flatten_outer_dims()
         first = 0
-        for h, width in enumerate((256, 256)):
+        for h, width in enumerate((192, 192, 128)):
             cols = slice(first, first + width)
             first = first + width
             staged = hold.tile([NQ, width], F32, name=f"staged{h}")

@@ -36,7 +36,7 @@ def tile_attend_spmm_kernel(tc, wT, vT, offs, out):
         windows = [pool01[:, 0, :], pool01[:, 1, :], late[0][:], late[1][:]]
         w_raw = hold.tile([P, PACK, NQ], F32, name="w_raw", align_bytes=64)
 
-        nc.sync.dma_start(out=pool01[:], in_=vT[:2 * P, :].rearrange("(b p) t -> p b t", b=2))
+        nc.sync.dma_start(out=pool01[:], in_=vT[:2 * P, :].rearrange("(p b) t -> p b t", b=2))
         nc.sync.dma_start(offsets[:], offs)
         for b in range(2, BLOCKS):
             nc.sync.dma_start(out=windows[b], in_=vT[b * P:(b + 1) * P, :])
@@ -109,10 +109,12 @@ def tile_attend_spmm_kernel(tc, wT, vT, offs, out):
             stop=True,
         )
         result = out.flatten_outer_dims()
-        first = 0
-        for h, width in enumerate((192, 192, 128)):
-            cols = slice(first, first + width)
-            first = first + width
-            staged = hold.tile([NQ, width], F32, name=f"staged{h}")
-            nc.vector.tensor_copy(staged[:], acc[:, cols])
-            nc.sync.dma_start(out=result[:, cols], in_=staged[:])
+        paired = acc[:, :2 * P].rearrange("q (b r) -> q r b", b=2)
+        staged = [hold.tile([NQ, width], F32, name=f"staged{h}") for h, width in enumerate((128, 192, 192))]
+        nc.vector.tensor_copy(staged[0][:].rearrange("q (r b) -> q r b", b=2), paired[:, :half, :])
+        nc.sync.dma_start(out=result[:, :128], in_=staged[0][:])
+        nc.vector.tensor_copy(staged[1][:, :P].rearrange("q (r b) -> q r b", b=2), paired[:, half:, :])
+        nc.vector.tensor_copy(staged[1][:, P:], acc[:, 256:320])
+        nc.sync.dma_start(out=result[:, 128:320], in_=staged[1][:])
+        nc.vector.tensor_copy(staged[2][:], acc[:, 320:])
+        nc.sync.dma_start(out=result[:, 320:], in_=staged[2][:])

@@ -42,7 +42,7 @@ def tile_attend_spmm_kernel(tc, wT, vT, offs, out):
             nc.sync.dma_start(out=windows[b], in_=vT[b * P:(b + 1) * P, :])
         nc.sync.dma_start(out=w_raw[:], in_=wT.flatten_outer_dims().rearrange("(p t) q -> p t q", t=PACK))
 
-        v_codes = hold.tile([P, DV], U32, name="v_codes", tag=f"pool{BLOCKS - 2}", align_bytes=64)
+        v_codes = hold.tile([P, DV], U32, name="v_codes", tag=f"pool{BLOCKS - 1}", align_bytes=64)
         v_scales = hold.tile([P, DV], U8, name="v_scales", align_bytes=64)
         w_codes = hold.tile([P, NQ], U32, name="w_codes", align_bytes=64)
         w_scales = hold.tile([P, NQ], U8, name="w_scales", align_bytes=64)
@@ -57,9 +57,9 @@ def tile_attend_spmm_kernel(tc, wT, vT, offs, out):
             for u in range(2):
                 nc.tensor.transpose(turned[b][:, u, :], words[:, u * P:(u + 1) * P], ident[:])
 
-        early = hold.tile([P, P, PACK], BF16, name="grouped0", align_bytes=64)
-        middle = hold.tile([P, 2 * P, PACK], BF16, name="grouped12", tag=f"pool{BLOCKS - 1}", align_bytes=64)
-        grouped = [early[:], middle[:, :P], middle[:, P:]]
+        early = hold.tile([P, 2 * P, PACK], BF16, name="grouped01", align_bytes=64)
+        grouped = [early[:, :P], early[:, P:]]
+        grouped.append(hold.tile([P, P, PACK], BF16, name="grouped2", align_bytes=64)[:])
         half = P // 2
         last_halves = [hold.tile([P, half, PACK], BF16, name=f"grouped3_{h}", align_bytes=64) for h in range(2)]
 
@@ -74,27 +74,26 @@ def tile_attend_spmm_kernel(tc, wT, vT, offs, out):
                 in_=source.rearrange("p r t -> p (r t)"),
             )
 
-        gather(0)
-        group(0)
-        gather(1)
-        gather(2)
-        quantize(0, P, early[:])
+        for b in range(BLOCKS - 2):
+            gather(b)
+            group(b)
+        gather(BLOCKS - 2)
+        group(BLOCKS - 2)
         gather(BLOCKS - 1)
+        quantize(0, 2 * P, early[:])
         w_grouped = hold.tile([P, NQ, PACK], BF16, name="w_grouped", align_bytes=64)
-        nc.vector.tensor_copy(out=w_grouped[:], in_=w_raw[:].rearrange("p t q -> p q t"))
-        group(1)
-        group(2)
+        nc.scalar.copy(out=w_grouped[:], in_=w_raw[:].rearrange("p t q -> p q t"))
         for h in range(2):
             nc.scalar.copy(
                 out=last_halves[h][:].bitcast(F32),
                 in_=turned[BLOCKS - 1][:, :, h * half:(h + 1) * half].rearrange("p u r -> p r u"),
             )
+        quantize(2 * P, 3 * P, grouped[2])
         nc.vector.quantize_mx(
             out=w_codes[:].bitcast(E5M2X4),
             scales=w_scales[:],
             in_=w_grouped[:].rearrange("p q t -> p (q t)"),
         )
-        quantize(P, 3 * P, middle[:])
         for h in range(2):
             quantize(3 * P + h * half, 3 * P + (h + 1) * half, last_halves[h][:])
 

@@ -61,7 +61,8 @@ def tile_attend_spmm_kernel(tc, wT, vT, offs, out):
         grouped = [early[:, :P], early[:, P:]]
         grouped.append(hold.tile([P, P, PACK], BF16, name="grouped2", align_bytes=64)[:])
         half = P // 2
-        last_halves = [hold.tile([P, half, PACK], BF16, name=f"grouped3_{h}", align_bytes=64) for h in range(2)]
+        last_cuts = ((0, 64), (64, 96), (96, 128))
+        last_parts = [hold.tile([P, b - a, PACK], BF16, name=f"grouped3_{a}", align_bytes=64) for a, b in last_cuts]
 
         def group(b):
             nc.scalar.copy(out=grouped[b].bitcast(F32), in_=turned[b][:].rearrange("p u r -> p r u"))
@@ -83,10 +84,10 @@ def tile_attend_spmm_kernel(tc, wT, vT, offs, out):
         quantize(0, 2 * P, early[:])
         w_grouped = hold.tile([P, NQ, PACK], BF16, name="w_grouped", align_bytes=64)
         nc.scalar.copy(out=w_grouped[:], in_=w_raw[:].rearrange("p t q -> p q t"))
-        for h in range(2):
+        for part, (a, b) in zip(last_parts, last_cuts):
             nc.scalar.copy(
-                out=last_halves[h][:].bitcast(F32),
-                in_=turned[BLOCKS - 1][:, :, h * half:(h + 1) * half].rearrange("p u r -> p r u"),
+                out=part[:].bitcast(F32),
+                in_=turned[BLOCKS - 1][:, :, a:b].rearrange("p u r -> p r u"),
             )
         quantize(2 * P, 3 * P, grouped[2])
         nc.vector.quantize_mx(
@@ -94,8 +95,8 @@ def tile_attend_spmm_kernel(tc, wT, vT, offs, out):
             scales=w_scales[:],
             in_=w_grouped[:].rearrange("p q t -> p (q t)"),
         )
-        for h in range(2):
-            quantize(3 * P + h * half, 3 * P + (h + 1) * half, last_halves[h][:])
+        for part, (a, b) in zip(last_parts, last_cuts):
+            quantize(3 * P + a, 3 * P + b, part[:])
 
         acc = psum.tile([NQ, DV], F32, name="acc")
         nc.tensor.matmul_mx(

@@ -48,24 +48,24 @@ def tile_attend_spmm_kernel(tc, wT, vT, offs, out):
         w_scales = hold.tile([P, NQ], U8, name="w_scales", align_bytes=64)
 
         turned = {}
+        turned01 = psum.tile([P, 2, 2, P], F32, name="turned01")
 
         def gather(b):
             picked = hold.tile([P, 2, P, 2], BF16, name=f"picked{b}", align_bytes=64)
             nc.vector.tensor_copy(picked[:].rearrange("d u p e -> d p u e"), windows[b].indirect(offsets[:]))
             words = picked[:].rearrange("d u p e -> d (u p e)").bitcast(F32)
-            turned[b] = psum.tile([P, 2, P], F32, name=f"turned{b}")
+            turned[b] = turned01[:, b] if b < 2 else psum.tile([P, 2, P], F32, name=f"turned{b}")[:]
             for u in range(2):
                 nc.tensor.transpose(turned[b][:, u, :], words[:, u * P:(u + 1) * P], ident[:])
 
         early = hold.tile([P, 2 * P, PACK], BF16, name="grouped01", align_bytes=64)
         grouped = [early[:, :P], early[:, P:]]
         grouped.append(hold.tile([P, P, PACK], BF16, name="grouped2", align_bytes=64)[:])
-        half = P // 2
         last_cuts = ((0, 64), (64, 96), (96, 128))
         last_parts = [hold.tile([P, b - a, PACK], BF16, name=f"grouped3_{a}", align_bytes=64) for a, b in last_cuts]
 
         def group(b):
-            nc.scalar.copy(out=grouped[b].bitcast(F32), in_=turned[b][:].rearrange("p u r -> p r u"))
+            nc.scalar.copy(out=grouped[b].bitcast(F32), in_=turned[b].rearrange("p u r -> p r u"))
 
         def quantize(first, last, source):
             cols = slice(first, last)
@@ -77,13 +77,19 @@ def tile_attend_spmm_kernel(tc, wT, vT, offs, out):
 
         for b in range(BLOCKS - 2):
             gather(b)
-            group(b)
+        nc.scalar.copy(
+            out=early[:].bitcast(F32).rearrange("p (r b) u -> p r b u", b=2),
+            in_=turned01[:].rearrange("p b u r -> p r b u"),
+        )
         gather(BLOCKS - 2)
         group(BLOCKS - 2)
         gather(BLOCKS - 1)
         quantize(0, 2 * P, early[:])
         w_grouped = hold.tile([P, NQ, PACK], BF16, name="w_grouped", align_bytes=64)
-        nc.scalar.copy(out=w_grouped[:], in_=w_raw[:].rearrange("p t q -> p q t"))
+        nc.scalar.copy(
+            out=w_grouped[:].rearrange("p (c i) t -> p c t i", i=4),
+            in_=w_raw[:].rearrange("p t (c i) -> p c t i", i=4),
+        )
         for part, (a, b) in zip(last_parts, last_cuts):
             nc.scalar.copy(
                 out=part[:].bitcast(F32),
@@ -109,12 +115,9 @@ def tile_attend_spmm_kernel(tc, wT, vT, offs, out):
             stop=True,
         )
         result = out.flatten_outer_dims()
-        paired = acc[:, :2 * P].rearrange("q (b r) -> q r b", b=2)
-        staged = [hold.tile([NQ, width], F32, name=f"staged{h}") for h, width in enumerate((128, 192, 192))]
-        nc.vector.tensor_copy(staged[0][:].rearrange("q (r b) -> q r b", b=2), paired[:, :half, :])
-        nc.sync.dma_start(out=result[:, :128], in_=staged[0][:])
-        nc.vector.tensor_copy(staged[1][:, :P].rearrange("q (r b) -> q r b", b=2), paired[:, half:, :])
-        nc.vector.tensor_copy(staged[1][:, P:], acc[:, 256:320])
-        nc.sync.dma_start(out=result[:, 128:320], in_=staged[1][:])
-        nc.vector.tensor_copy(staged[2][:], acc[:, 320:])
-        nc.sync.dma_start(out=result[:, 320:], in_=staged[2][:])
+        first = 0
+        for h, width in enumerate((128, 192, 192)):
+            staged = hold.tile([NQ, width], F32, name=f"staged{h}")
+            nc.scalar.copy(out=staged[:], in_=acc[:, first:first + width])
+            nc.sync.dma_start(out=result[:, first:first + width], in_=staged[:])
+            first = first + width

@@ -116,7 +116,7 @@ def tile_attend_spmm_kernel(tc, wT, vT, offs, out):
         )
         result = out.flatten_outer_dims()
         first = 0
-        for h, width in enumerate((128, 192, 192)):
+        for h, width in enumerate((128, 160, 224)):
             staged = hold.tile([NQ, width], F32, name=f"staged{h}")
             nc.scalar.copy(out=staged[:], in_=acc[:, first:first + width])
             nc.sync.dma_start(out=result[:, first:first + width], in_=staged[:])

@@ -8,7 +8,15 @@ FLOPS = 2 * N * NQ * DV
 
 P = 128
 PACK = 4
-BLOCKS = DV // P
+PARTS = DV // P
+PAIRED = 2
+LAST = PARTS - 1
+LINE = 4
+LIST_ROWS = 16
+
+LAST_CUTS = tuple((begin, begin + 32) for begin in range(0, P, 32))
+
+STORE_WIDTHS = (128, 160, 224)
 
 F32 = mybir.dt.float32
 BF16 = mybir.dt.bfloat16
@@ -30,79 +38,78 @@ def tile_attend_spmm_kernel(tc, wT, vT, offs, out):
         ident = hold.tile([P, P], F32, name="ident")
         nc.scalar.copy(out=ident[:], in_=ident_made[:])
 
-        offsets = hold.tile([P, N // 16], U16, name="offsets")
-        pool01 = hold.tile([P, 2, T], F32, name="pool01", align_bytes=64)
-        late = [hold.tile([P, T], F32, name=f"pool_v{b}", tag=f"pool{b}", align_bytes=64) for b in range(2, BLOCKS)]
-        windows = [pool01[:, 0, :], pool01[:, 1, :], late[0][:], late[1][:]]
+        offsets = hold.tile([P, N // LIST_ROWS], U16, name="offsets")
+        pool01 = hold.tile([P, PAIRED, T], F32, name="pool01", align_bytes=64)
+        late = [hold.tile([P, T], F32, name=f"pool_v{b}", tag=f"pool{b}", align_bytes=64) for b in range(PAIRED, PARTS)]
+        windows = [pool01[:, b, :] for b in range(PAIRED)] + [tile[:] for tile in late]
         w_raw = hold.tile([P, PACK, NQ], F32, name="w_raw", align_bytes=64)
 
-        nc.sync.dma_start(out=pool01[:], in_=vT[:2 * P, :].rearrange("(p b) t -> p b t", b=2))
+        nc.sync.dma_start(out=pool01[:], in_=vT[:PAIRED * P, :].rearrange("(p b) t -> p b t", b=PAIRED))
         nc.sync.dma_start(offsets[:], offs)
-        for b in range(2, BLOCKS):
+        for b in range(PAIRED, PARTS):
             nc.sync.dma_start(out=windows[b], in_=vT[b * P:(b + 1) * P, :])
         nc.sync.dma_start(out=w_raw[:], in_=wT.flatten_outer_dims().rearrange("(p t) q -> p t q", t=PACK))
 
-        v_codes = hold.tile([P, DV], U32, name="v_codes", tag=f"pool{BLOCKS - 1}", align_bytes=64)
+        v_codes = hold.tile([P, DV], U32, name="v_codes", tag=f"pool{LAST}", align_bytes=64)
         v_scales = hold.tile([P, DV], U8, name="v_scales", align_bytes=64)
         w_codes = hold.tile([P, NQ], U32, name="w_codes", align_bytes=64)
         w_scales = hold.tile([P, NQ], U8, name="w_scales", align_bytes=64)
 
-        turned = {}
-        turned01 = psum.tile([P, 2, 2, P], F32, name="turned01")
+        turned01 = psum.tile([P, PAIRED, 2, P], F32, name="turned01")
 
-        def gather(b):
+        def gather_and_turn(b):
             picked = hold.tile([P, 2, P, 2], BF16, name=f"picked{b}", align_bytes=64)
             nc.vector.tensor_copy(picked[:].rearrange("d u p e -> d p u e"), windows[b].indirect(offsets[:]))
             words = picked[:].rearrange("d u p e -> d (u p e)").bitcast(F32)
-            turned[b] = turned01[:, b] if b < 2 else psum.tile([P, 2, P], F32, name=f"turned{b}")[:]
+            turned = turned01[:, b] if b < PAIRED else psum.tile([P, 2, P], F32, name=f"turned{b}")[:]
             for u in range(2):
-                nc.tensor.transpose(turned[b][:, u, :], words[:, u * P:(u + 1) * P], ident[:])
+                nc.tensor.transpose(turned[:, u, :], words[:, u * P:(u + 1) * P], ident[:])
+            return turned
 
-        early = hold.tile([P, 2 * P, PACK], BF16, name="grouped01", align_bytes=64)
-        grouped = [early[:, :P], early[:, P:]]
-        grouped.append(hold.tile([P, P, PACK], BF16, name="grouped2", align_bytes=64)[:])
-        last_cuts = ((0, 64), (64, 96), (96, 128))
-        last_parts = [hold.tile([P, b - a, PACK], BF16, name=f"grouped3_{a}", align_bytes=64) for a, b in last_cuts]
+        grouped01 = hold.tile([P, PAIRED * P, PACK], BF16, name="grouped01", align_bytes=64)
+        grouped2 = hold.tile([P, P, PACK], BF16, name="grouped2", align_bytes=64)
+        last_pieces = [
+            hold.tile([P, end - begin, PACK], BF16, name=f"grouped3_{begin}", align_bytes=64)
+            for begin, end in LAST_CUTS
+        ]
 
-        def group(b):
-            nc.scalar.copy(out=grouped[b].bitcast(F32), in_=turned[b].rearrange("p u r -> p r u"))
+        def group(grouped, turned):
+            nc.scalar.copy(out=grouped[:].bitcast(F32), in_=turned.rearrange("p u r -> p r u"))
 
-        def quantize(first, last, source):
-            cols = slice(first, last)
+        def quantize_values(first, grouped):
+            cols = slice(first, first + grouped.shape[1])
             nc.vector.quantize_mx(
                 out=v_codes[:, cols].bitcast(E4M3X4),
                 scales=v_scales[:, cols],
-                in_=source.rearrange("p r t -> p (r t)"),
+                in_=grouped[:].rearrange("p r t -> p (r t)"),
             )
 
-        for b in range(BLOCKS - 2):
-            gather(b)
+        for b in range(PAIRED):
+            gather_and_turn(b)
         nc.scalar.copy(
-            out=early[:].bitcast(F32).rearrange("p (r b) u -> p r b u", b=2),
+            out=grouped01[:].bitcast(F32).rearrange("p (r b) u -> p r b u", b=PAIRED),
             in_=turned01[:].rearrange("p b u r -> p r b u"),
         )
-        gather(BLOCKS - 2)
-        group(BLOCKS - 2)
-        gather(BLOCKS - 1)
-        quantize(0, 2 * P, early[:])
+        group(grouped2, gather_and_turn(PAIRED))
+        turned_last = gather_and_turn(LAST)
+        quantize_values(0, grouped01)
+
         w_grouped = hold.tile([P, NQ, PACK], BF16, name="w_grouped", align_bytes=64)
         nc.scalar.copy(
-            out=w_grouped[:].rearrange("p (c i) t -> p c t i", i=4),
-            in_=w_raw[:].rearrange("p t (c i) -> p c t i", i=4),
+            out=w_grouped[:].rearrange("p (c i) t -> p c t i", i=LINE),
+            in_=w_raw[:].rearrange("p t (c i) -> p c t i", i=LINE),
         )
-        for part, (a, b) in zip(last_parts, last_cuts):
-            nc.scalar.copy(
-                out=part[:].bitcast(F32),
-                in_=turned[BLOCKS - 1][:, :, a:b].rearrange("p u r -> p r u"),
-            )
-        quantize(2 * P, 3 * P, grouped[2])
+        for piece, (begin, end) in zip(last_pieces, LAST_CUTS):
+            group(piece, turned_last[:, :, begin:end])
+
+        quantize_values(PAIRED * P, grouped2)
         nc.vector.quantize_mx(
             out=w_codes[:].bitcast(E5M2X4),
             scales=w_scales[:],
             in_=w_grouped[:].rearrange("p q t -> p (q t)"),
         )
-        for part, (a, b) in zip(last_parts, last_cuts):
-            quantize(3 * P + a, 3 * P + b, part[:])
+        for piece, (begin, end) in zip(last_pieces, LAST_CUTS):
+            quantize_values(LAST * P + begin, piece)
 
         acc = psum.tile([NQ, DV], F32, name="acc")
         nc.tensor.matmul_mx(
@@ -114,9 +121,10 @@ def tile_attend_spmm_kernel(tc, wT, vT, offs, out):
             start=True,
             stop=True,
         )
+
         result = out.flatten_outer_dims()
         first = 0
-        for h, width in enumerate((128, 160, 224)):
+        for h, width in enumerate(STORE_WIDTHS):
             staged = hold.tile([NQ, width], F32, name=f"staged{h}")
             nc.scalar.copy(out=staged[:], in_=acc[:, first:first + width])
             nc.sync.dma_start(out=result[:, first:first + width], in_=staged[:])

@@ -33,10 +33,8 @@ def tile_attend_spmm_kernel(tc, wT, vT, offs, out):
         hold = ctx.enter_context(tc.tile_pool(name="hold", bufs=1))
         psum = ctx.enter_context(tc.psum_pool(name="psum", bufs=1))
 
-        ident_made = hold.tile([P, P], F32, name="ident_made")
-        make_identity(nc, ident_made[:])
         ident = hold.tile([P, P], F32, name="ident")
-        nc.scalar.copy(out=ident[:], in_=ident_made[:])
+        make_identity(nc, ident[:])
 
         offsets = hold.tile([P, N // LIST_ROWS], U16, name="offsets")
         pool01 = hold.tile([P, PAIRED, T], F32, name="pool01", align_bytes=64)

@@ -37,10 +37,10 @@ def tile_attend_spmm_kernel(tc, wT, vT, offs, out):
         make_identity(nc, ident[:])
 
         offsets = hold.tile([P, N // LIST_ROWS], U16, name="offsets")
-        pool01 = hold.tile([P, PAIRED, T], F32, name="pool01", align_bytes=64)
-        late = [hold.tile([P, T], F32, name=f"pool_v{b}", tag=f"pool{b}", align_bytes=64) for b in range(PAIRED, PARTS)]
+        pool01 = hold.tile([P, PAIRED, T], F32, name="pool01", align_bytes=256)
+        late = [hold.tile([P, T], F32, name=f"pool_v{b}", tag=f"pool{b}", align_bytes=256) for b in range(PAIRED, PARTS)]
         windows = [pool01[:, b, :] for b in range(PAIRED)] + [tile[:] for tile in late]
-        w_raw = hold.tile([P, PACK, NQ], F32, name="w_raw", align_bytes=64)
+        w_raw = hold.tile([P, PACK, NQ], F32, name="w_raw", align_bytes=256)
 
         nc.sync.dma_start(out=pool01[:], in_=vT[:PAIRED * P, :].rearrange("(p b) t -> p b t", b=PAIRED))
         nc.sync.dma_start(offsets[:], offs)
@@ -48,7 +48,7 @@ def tile_attend_spmm_kernel(tc, wT, vT, offs, out):
             nc.sync.dma_start(out=windows[b], in_=vT[b * P:(b + 1) * P, :])
         nc.sync.dma_start(out=w_raw[:], in_=wT.flatten_outer_dims().rearrange("(p t) q -> p t q", t=PACK))
 
-        v_codes = hold.tile([P, DV], U32, name="v_codes", tag=f"pool{LAST}", align_bytes=64)
+        v_codes = hold.tile([P, DV], U32, name="v_codes", tag=f"pool{LAST}", align_bytes=256)
         v_scales = hold.tile([P, DV], U8, name="v_scales", align_bytes=64)
         w_codes = hold.tile([P, NQ], U32, name="w_codes", align_bytes=64)
         w_scales = hold.tile([P, NQ], U8, name="w_scales", align_bytes=64)
@@ -121,9 +121,10 @@ def tile_attend_spmm_kernel(tc, wT, vT, offs, out):
         )
 
         result = out.flatten_outer_dims()
+        staged = hold.tile([NQ, DV], F32, name="staged", align_bytes=256)
         first = 0
-        for h, width in enumerate(STORE_WIDTHS):
-            staged = hold.tile([NQ, width], F32, name=f"staged{h}")
-            nc.scalar.copy(out=staged[:], in_=acc[:, first:first + width])
-            nc.sync.dma_start(out=result[:, first:first + width], in_=staged[:])
+        for width in STORE_WIDTHS:
+            cols = slice(first, first + width)
+            nc.scalar.copy(out=staged[:, cols], in_=acc[:, cols])
+            nc.sync.dma_start(out=result[:, cols], in_=staged[:, cols])
             first = first + width

@@ -16,7 +16,7 @@ LIST_ROWS = 16
 
 LAST_CUTS = tuple((begin, begin + 32) for begin in range(0, P, 32))
 
-STORE_WIDTHS = (128, 160, 224)
+STORE_WIDTHS = (128, 192, 192)
 
 F32 = mybir.dt.float32
 BF16 = mybir.dt.bfloat16

@@ -12,6 +12,7 @@ PARTS = DV // P
 PAIRED = 2
 LAST = PARTS - 1
 LINE = 4
+DMA_ALIGN = 256
 LIST_ROWS = 16
 
 LAST_CUTS = tuple((begin, begin + 32) for begin in range(0, P, 32))
@@ -33,14 +34,17 @@ def tile_attend_spmm_kernel(tc, wT, vT, offs, out):
         hold = ctx.enter_context(tc.tile_pool(name="hold", bufs=1))
         psum = ctx.enter_context(tc.psum_pool(name="psum", bufs=1))
 
-        ident = hold.tile([P, P], F32, name="ident")
+        ident = hold.tile([P, P], F32, name="ident", align_bytes=DMA_ALIGN)
         make_identity(nc, ident[:])
 
         offsets = hold.tile([P, N // LIST_ROWS], U16, name="offsets")
-        pool01 = hold.tile([P, PAIRED, T], F32, name="pool01", align_bytes=256)
-        late = [hold.tile([P, T], F32, name=f"pool_v{b}", tag=f"pool{b}", align_bytes=256) for b in range(PAIRED, PARTS)]
+        pool01 = hold.tile([P, PAIRED, T], F32, name="pool01", align_bytes=DMA_ALIGN)
+        late = [
+            hold.tile([P, T], F32, name=f"pool_v{b}", tag=f"pool{b}", align_bytes=DMA_ALIGN)
+            for b in range(PAIRED, PARTS)
+        ]
         windows = [pool01[:, b, :] for b in range(PAIRED)] + [tile[:] for tile in late]
-        w_raw = hold.tile([P, PACK, NQ], F32, name="w_raw", align_bytes=256)
+        w_raw = hold.tile([P, PACK, NQ], F32, name="w_raw", align_bytes=DMA_ALIGN)
 
         nc.sync.dma_start(out=pool01[:], in_=vT[:PAIRED * P, :].rearrange("(p b) t -> p b t", b=PAIRED))
         nc.sync.dma_start(offsets[:], offs)
@@ -48,15 +52,15 @@ def tile_attend_spmm_kernel(tc, wT, vT, offs, out):
             nc.sync.dma_start(out=windows[b], in_=vT[b * P:(b + 1) * P, :])
         nc.sync.dma_start(out=w_raw[:], in_=wT.flatten_outer_dims().rearrange("(p t) q -> p t q", t=PACK))
 
-        v_codes = hold.tile([P, DV], U32, name="v_codes", tag=f"pool{LAST}", align_bytes=256)
-        v_scales = hold.tile([P, DV], U8, name="v_scales", align_bytes=64)
-        w_codes = hold.tile([P, NQ], U32, name="w_codes", align_bytes=64)
-        w_scales = hold.tile([P, NQ], U8, name="w_scales", align_bytes=64)
+        v_codes = hold.tile([P, DV], U32, name="v_codes", tag=f"pool{LAST}", align_bytes=DMA_ALIGN)
+        v_scales = hold.tile([P, DV], U8, name="v_scales", align_bytes=DMA_ALIGN)
+        w_codes = hold.tile([P, NQ], U32, name="w_codes", align_bytes=DMA_ALIGN)
+        w_scales = hold.tile([P, NQ], U8, name="w_scales", align_bytes=DMA_ALIGN)
 
         turned01 = psum.tile([P, PAIRED, 2, P], F32, name="turned01")
 
         def gather_and_turn(b):
-            picked = hold.tile([P, 2, P, 2], BF16, name=f"picked{b}", align_bytes=64)
+            picked = hold.tile([P, 2, P, 2], BF16, name=f"picked{b}", align_bytes=DMA_ALIGN)
             nc.vector.tensor_copy(picked[:].rearrange("d u p e -> d p u e"), windows[b].indirect(offsets[:]))
             words = picked[:].rearrange("d u p e -> d (u p e)").bitcast(F32)
             turned = turned01[:, b] if b < PAIRED else psum.tile([P, 2, P], F32, name=f"turned{b}")[:]
@@ -64,10 +68,10 @@ def tile_attend_spmm_kernel(tc, wT, vT, offs, out):
                 nc.tensor.transpose(turned[:, u, :], words[:, u * P:(u + 1) * P], ident[:])
             return turned
 
-        grouped01 = hold.tile([P, PAIRED * P, PACK], BF16, name="grouped01", align_bytes=64)
-        grouped2 = hold.tile([P, P, PACK], BF16, name="grouped2", align_bytes=64)
+        grouped01 = hold.tile([P, PAIRED * P, PACK], BF16, name="grouped01", align_bytes=DMA_ALIGN)
+        grouped2 = hold.tile([P, P, PACK], BF16, name="grouped2", align_bytes=DMA_ALIGN)
         last_pieces = [
-            hold.tile([P, end - begin, PACK], BF16, name=f"grouped3_{begin}", align_bytes=64)
+            hold.tile([P, end - begin, PACK], BF16, name=f"grouped3_{begin}", align_bytes=DMA_ALIGN)
             for begin, end in LAST_CUTS
         ]
 
@@ -92,7 +96,7 @@ def tile_attend_spmm_kernel(tc, wT, vT, offs, out):
         turned_last = gather_and_turn(LAST)
         quantize_values(0, grouped01)
 
-        w_grouped = hold.tile([P, NQ, PACK], BF16, name="w_grouped", align_bytes=64)
+        w_grouped = hold.tile([P, NQ, PACK], BF16, name="w_grouped", align_bytes=DMA_ALIGN)
         nc.scalar.copy(
             out=w_grouped[:].rearrange("p (c i) t -> p c t i", i=LINE),
             in_=w_raw[:].rearrange("p t (c i) -> p c t i", i=LINE),
@@ -121,7 +125,7 @@ def tile_attend_spmm_kernel(tc, wT, vT, offs, out):
         )
 
         result = out.flatten_outer_dims()
-        staged = hold.tile([NQ, DV], F32, name="staged", align_bytes=256)
+        staged = hold.tile([NQ, DV], F32, name="staged", align_bytes=DMA_ALIGN)
         first = 0
         for width in STORE_WIDTHS:
             cols = slice(first, first + width)

@@ -14,10 +14,8 @@ LAST = PARTS - 1
 LINE = 4
 DMA_ALIGN = 256
 LIST_ROWS = 16
-
+VECTOR_SLOTS = 288
 LAST_CUTS = tuple((begin, begin + 32) for begin in range(0, P, 32))
-
-STORE_WIDTHS = (128, 192, 192)
 
 F32 = mybir.dt.float32
 BF16 = mybir.dt.bfloat16
@@ -26,6 +24,7 @@ U16 = mybir.dt.uint16
 U8 = mybir.dt.uint8
 E4M3X4 = mybir.dt.float8_e4m3fn_x4
 E5M2X4 = mybir.dt.float8_e5m2_x4
+COPY = mybir.ActivationFunctionType.Copy
 
 
 def tile_attend_spmm_kernel(tc, wT, vT, offs, out):
@@ -38,97 +37,99 @@ def tile_attend_spmm_kernel(tc, wT, vT, offs, out):
         make_identity(nc, ident[:])
 
         offsets = hold.tile([P, N // LIST_ROWS], U16, name="offsets")
-        pool01 = hold.tile([P, PAIRED, T], F32, name="pool01", align_bytes=DMA_ALIGN)
-        late = [
-            hold.tile([P, T], F32, name=f"pool_v{b}", tag=f"pool{b}", align_bytes=DMA_ALIGN)
-            for b in range(PAIRED, PARTS)
+        pools = [
+            hold.tile([P, T], F32, name=f"pool_v{b}", tag=f"pool{b}", align_bytes=DMA_ALIGN) for b in range(PARTS)
         ]
-        windows = [pool01[:, b, :] for b in range(PAIRED)] + [tile[:] for tile in late]
+        windows = [tile[:] for tile in pools]
         w_raw = hold.tile([P, PACK, NQ], F32, name="w_raw", align_bytes=DMA_ALIGN)
 
-        nc.sync.dma_start(out=pool01[:], in_=vT[:PAIRED * P, :].rearrange("(p b) t -> p b t", b=PAIRED))
+        nc.sync.dma_start(out=windows[0], in_=vT[:P, :])
         nc.sync.dma_start(offsets[:], offs)
-        for b in range(PAIRED, PARTS):
+        for b in range(1, LAST):
             nc.sync.dma_start(out=windows[b], in_=vT[b * P:(b + 1) * P, :])
         nc.sync.dma_start(out=w_raw[:], in_=wT.flatten_outer_dims().rearrange("(p t) q -> p t q", t=PACK))
+        nc.sync.dma_start(out=windows[LAST], in_=vT[LAST * P:, :])
 
-        v_codes = hold.tile([P, DV], U32, name="v_codes", tag=f"pool{LAST}", align_bytes=DMA_ALIGN)
-        v_scales = hold.tile([P, DV], U8, name="v_scales", align_bytes=DMA_ALIGN)
+        early_codes = hold.tile([P, LAST * P], U32, name="early_codes", align_bytes=DMA_ALIGN)
+        early_scales = hold.tile([P, LAST * P], U8, name="early_scales", align_bytes=DMA_ALIGN)
+        last_codes = hold.tile([P, P], U32, name="last_codes", align_bytes=DMA_ALIGN)
+        last_scales = hold.tile([P, P], U8, name="last_scales", align_bytes=DMA_ALIGN)
         w_codes = hold.tile([P, NQ], U32, name="w_codes", align_bytes=DMA_ALIGN)
         w_scales = hold.tile([P, NQ], U8, name="w_scales", align_bytes=DMA_ALIGN)
 
-        turned01 = psum.tile([P, PAIRED, 2, P], F32, name="turned01")
-
         def gather_and_turn(b):
-            picked = hold.tile([P, 2, P, 2], BF16, name=f"picked{b}", align_bytes=DMA_ALIGN)
-            nc.vector.tensor_copy(picked[:].rearrange("d u p e -> d p u e"), windows[b].indirect(offsets[:]))
-            words = picked[:].rearrange("d u p e -> d (u p e)").bitcast(F32)
-            turned = turned01[:, b] if b < PAIRED else psum.tile([P, 2, P], F32, name=f"turned{b}")[:]
+            picked = hold.tile([P, N], BF16, name=f"picked{b}", align_bytes=DMA_ALIGN)
+            cut = VECTOR_SLOTS // LIST_ROWS
+            nc.vector.tensor_copy(picked[:, :VECTOR_SLOTS], windows[b].indirect(offsets[:, :cut]))
+            nc.scalar.activation(picked[:, VECTOR_SLOTS:], windows[b].indirect(offsets[:, cut:]), COPY)
+            words = picked[:].bitcast(F32)
+            turned = psum.tile([P, 2, P], F32, name=f"turned{b}")
             for u in range(2):
-                nc.tensor.transpose(turned[:, u, :], words[:, u * P:(u + 1) * P], ident[:])
+                nc.tensor.transpose(turned[:, u, :], words[:, u::2], ident[:])
             return turned
 
-        grouped01 = hold.tile([P, PAIRED * P, PACK], BF16, name="grouped01", align_bytes=DMA_ALIGN)
-        grouped2 = hold.tile([P, P, PACK], BF16, name="grouped2", align_bytes=DMA_ALIGN)
-        last_pieces = [
-            hold.tile([P, end - begin, PACK], BF16, name=f"grouped3_{begin}", align_bytes=DMA_ALIGN)
-            for begin, end in LAST_CUTS
-        ]
-
         def group(grouped, turned):
-            nc.scalar.copy(out=grouped[:].bitcast(F32), in_=turned.rearrange("p u r -> p r u"))
+            nc.scalar.copy(out=grouped.bitcast(F32), in_=turned.rearrange("p u r -> p r u"))
 
-        def quantize_values(first, grouped):
+        def quantize_values(codes, scales, first, grouped):
             cols = slice(first, first + grouped.shape[1])
             nc.vector.quantize_mx(
-                out=v_codes[:, cols].bitcast(E4M3X4),
-                scales=v_scales[:, cols],
-                in_=grouped[:].rearrange("p r t -> p (r t)"),
+                out=codes[:, cols].bitcast(E4M3X4),
+                scales=scales[:, cols],
+                in_=grouped.rearrange("p r t -> p (r t)"),
             )
 
-        for b in range(PAIRED):
-            gather_and_turn(b)
-        nc.scalar.copy(
-            out=grouped01[:].bitcast(F32).rearrange("p (r b) u -> p r b u", b=PAIRED),
-            in_=turned01[:].rearrange("p b u r -> p r b u"),
-        )
-        group(grouped2, gather_and_turn(PAIRED))
-        turned_last = gather_and_turn(LAST)
-        quantize_values(0, grouped01)
+        def multiply(acc, codes, scales):
+            nc.tensor.matmul_mx(
+                out=acc,
+                lhsT=w_codes[:].bitcast(E5M2X4),
+                lhsT_scale=w_scales[:],
+                rhs=codes.bitcast(E4M3X4),
+                rhs_scale=scales,
+                start=True,
+                stop=True,
+            )
+
+        for b in range(LAST):
+            grouped = hold.tile([P, P, PACK], BF16, name=f"grouped{b}", align_bytes=DMA_ALIGN)
+            group(grouped[:], gather_and_turn(b)[:])
+            quantize_values(early_codes, early_scales, b * P, grouped[:])
 
         w_grouped = hold.tile([P, NQ, PACK], BF16, name="w_grouped", align_bytes=DMA_ALIGN)
         nc.scalar.copy(
             out=w_grouped[:].rearrange("p (c i) t -> p c t i", i=LINE),
             in_=w_raw[:].rearrange("p t (c i) -> p c t i", i=LINE),
         )
-        for piece, (begin, end) in zip(last_pieces, LAST_CUTS):
-            group(piece, turned_last[:, :, begin:end])
-
-        quantize_values(PAIRED * P, grouped2)
         nc.vector.quantize_mx(
             out=w_codes[:].bitcast(E5M2X4),
             scales=w_scales[:],
             in_=w_grouped[:].rearrange("p q t -> p (q t)"),
         )
-        for piece, (begin, end) in zip(last_pieces, LAST_CUTS):
-            quantize_values(LAST * P + begin, piece)
-
-        acc = psum.tile([NQ, DV], F32, name="acc")
-        nc.tensor.matmul_mx(
-            out=acc[:],
-            lhsT=w_codes[:].bitcast(E5M2X4),
-            lhsT_scale=w_scales[:],
-            rhs=v_codes[:].bitcast(E4M3X4),
-            rhs_scale=v_scales[:],
-            start=True,
-            stop=True,
-        )
 
         result = out.flatten_outer_dims()
-        staged = hold.tile([NQ, DV], F32, name="staged", align_bytes=DMA_ALIGN)
-        first = 0
-        for width in STORE_WIDTHS:
-            cols = slice(first, first + width)
-            nc.scalar.copy(out=staged[:, cols], in_=acc[:, cols])
-            nc.sync.dma_start(out=result[:, cols], in_=staged[:, cols])
-            first = first + width
+        pair = PAIRED * P
+        acc01 = psum.tile([NQ, pair], F32, name="acc01")
+        acc2 = psum.tile([NQ, P], F32, name="acc2")
+        multiply(acc01[:], early_codes[:, :pair], early_scales[:, :pair])
+        multiply(acc2[:], early_codes[:, pair:], early_scales[:, pair:])
+
+        turned_last = gather_and_turn(LAST)
+
+        staged = hold.tile([NQ, LAST * P], F32, name="staged", tag=f"pool{LAST}", align_bytes=DMA_ALIGN)
+        nc.vector.tensor_copy(staged[:, :pair], acc01[:])
+        nc.vector.tensor_copy(staged[:, pair:], acc2[:])
+        nc.sync.dma_start(out=result[:, :LAST * P], in_=staged[:])
+
+        last_pieces = [
+            hold.tile([P, end - begin, PACK], BF16, name=f"grouped3_{begin}", align_bytes=DMA_ALIGN)
+            for begin, end in LAST_CUTS
+        ]
+        for piece, (begin, end) in zip(last_pieces, LAST_CUTS):
+            group(piece[:], turned_last[:, :, begin:end])
+        for piece, (begin, end) in zip(last_pieces, LAST_CUTS):
+            quantize_values(last_codes, last_scales, begin, piece[:])
+        acc3 = psum.tile([NQ, P], F32, name="acc3")
+        multiply(acc3[:], last_codes[:], last_scales[:])
+        staged_last = hold.tile([NQ, P], F32, name="staged_last", align_bytes=DMA_ALIGN)
+        nc.scalar.copy(out=staged_last[:], in_=acc3[:])
+        nc.sync.dma_start(out=result[:, LAST * P:], in_=staged_last[:])

@@ -1,7 +1,6 @@
 from contextlib import ExitStack
 
 import concourse.mybir as mybir
-from concourse.masks import make_identity
 
 N, T, DV, NQ = 512, 2048, 512, 128
 FLOPS = 2 * N * NQ * DV
@@ -31,27 +30,37 @@ def tile_attend_spmm_kernel(tc, wT, vT, offs, out):
     nc = tc.nc
     with ExitStack() as ctx:
         hold = ctx.enter_context(tc.tile_pool(name="hold", bufs=1))
+        placed = ctx.enter_context(tc.tile_pool(name="placed", bufs=1))
         psum = ctx.enter_context(tc.psum_pool(name="psum", bufs=1))
 
         ident = hold.tile([P, P], F32, name="ident", align_bytes=DMA_ALIGN)
-        make_identity(nc, ident[:])
+        zeros = hold.tile([P, P], F32, name="zeros", align_bytes=DMA_ALIGN)
+        nc.vector.memset(zeros[:], 0.0)
+        nc.scalar.copy(out=ident[:], in_=zeros[:])
+        nc.gpsimd.affine_select(
+            out=ident[:], in_=ident[:], compare_op=mybir.AluOpType.not_equal, fill=1.0, base=0,
+            pattern=[[-1, P]], channel_multiplier=1,
+        )
 
         offsets = hold.tile([P, N // LIST_ROWS], U16, name="offsets")
         pools = [
-            hold.tile([P, T], F32, name=f"pool_v{b}", tag=f"pool{b}", align_bytes=DMA_ALIGN) for b in range(PARTS)
+            hold.tile([P, T], F32, name=f"pool_v{b}", tag=f"pool{b}", align_bytes=DMA_ALIGN) for b in range(LAST)
         ]
+        pools.append(placed.tile([P, T], F32, name="pool_last", offset=0, align_bytes=DMA_ALIGN))
         windows = [tile[:] for tile in pools]
-        w_raw = hold.tile([P, PACK, NQ], F32, name="w_raw", align_bytes=DMA_ALIGN)
+        w_raw = hold.tile([P, PACK, NQ], F32, name="w_raw", tag="w_raw", align_bytes=DMA_ALIGN)
 
         nc.sync.dma_start(out=windows[0], in_=vT[:P, :])
         nc.sync.dma_start(offsets[:], offs)
         for b in range(1, LAST):
             nc.sync.dma_start(out=windows[b], in_=vT[b * P:(b + 1) * P, :])
-        nc.sync.dma_start(out=w_raw[:], in_=wT.flatten_outer_dims().rearrange("(p t) q -> p t q", t=PACK))
         nc.sync.dma_start(out=windows[LAST], in_=vT[LAST * P:, :])
+        nc.sync.dma_start(out=w_raw[:], in_=wT.flatten_outer_dims().rearrange("(p t) q -> p t q", t=PACK))
 
-        early_codes = hold.tile([P, LAST * P], U32, name="early_codes", align_bytes=DMA_ALIGN)
-        early_scales = hold.tile([P, LAST * P], U8, name="early_scales", align_bytes=DMA_ALIGN)
+        codes01 = hold.tile([P, PAIRED * P], U32, name="codes01", tag=f"pool{PAIRED}", align_bytes=DMA_ALIGN)
+        codes2 = placed.tile([P, P], U32, name="codes2", offset=0, align_bytes=DMA_ALIGN)
+        scales2 = hold.tile([P, P], U8, name="scales2", align_bytes=DMA_ALIGN)
+        early_scales = hold.tile([P, PAIRED * P], U8, name="early_scales", align_bytes=DMA_ALIGN)
         last_codes = hold.tile([P, P], U32, name="last_codes", align_bytes=DMA_ALIGN)
         last_scales = hold.tile([P, P], U8, name="last_scales", align_bytes=DMA_ALIGN)
         w_codes = hold.tile([P, NQ], U32, name="w_codes", align_bytes=DMA_ALIGN)
@@ -90,16 +99,20 @@ def tile_attend_spmm_kernel(tc, wT, vT, offs, out):
                 stop=True,
             )
 
+        grouped = [hold.tile([P, P, PACK], BF16, name=f"grouped{b}", align_bytes=DMA_ALIGN) for b in range(LAST)]
         for b in range(LAST):
-            grouped = hold.tile([P, P, PACK], BF16, name=f"grouped{b}", align_bytes=DMA_ALIGN)
-            group(grouped[:], gather_and_turn(b)[:])
-            quantize_values(early_codes, early_scales, b * P, grouped[:])
+            group(grouped[b][:], gather_and_turn(b)[:])
+        for b in range(PAIRED):
+            quantize_values(codes01, early_scales, b * P, grouped[b][:])
 
-        w_grouped = hold.tile([P, NQ, PACK], BF16, name="w_grouped", align_bytes=DMA_ALIGN)
-        nc.scalar.copy(
-            out=w_grouped[:].rearrange("p (c i) t -> p c t i", i=LINE),
-            in_=w_raw[:].rearrange("p t (c i) -> p c t i", i=LINE),
-        )
+        turned_last = gather_and_turn(LAST)
+
+        w_grouped = placed.tile([P, NQ, PACK], BF16, name="w_grouped", offset=1024, align_bytes=DMA_ALIGN)
+        w_out = w_grouped[:].rearrange("p (c i) t -> p c t i", i=LINE)
+        w_in = w_raw[:].rearrange("p t (c i) -> p c t i", i=LINE)
+        nc.vector.tensor_copy(w_out[:, :20], w_in[:, :20])
+        nc.scalar.copy(out=w_out[:, 20:], in_=w_in[:, 20:])
+        quantize_values(codes2, scales2, 0, grouped[PAIRED][:])
         nc.vector.quantize_mx(
             out=w_codes[:].bitcast(E5M2X4),
             scales=w_scales[:],
@@ -110,18 +123,14 @@ def tile_attend_spmm_kernel(tc, wT, vT, offs, out):
         pair = PAIRED * P
         acc01 = psum.tile([NQ, pair], F32, name="acc01")
         acc2 = psum.tile([NQ, P], F32, name="acc2")
-        multiply(acc01[:], early_codes[:, :pair], early_scales[:, :pair])
-        multiply(acc2[:], early_codes[:, pair:], early_scales[:, pair:])
-
-        turned_last = gather_and_turn(LAST)
-
-        staged = hold.tile([NQ, LAST * P], F32, name="staged", tag=f"pool{LAST}", align_bytes=DMA_ALIGN)
-        nc.vector.tensor_copy(staged[:, :pair], acc01[:])
-        nc.vector.tensor_copy(staged[:, pair:], acc2[:])
-        nc.sync.dma_start(out=result[:, :LAST * P], in_=staged[:])
+        multiply(acc01[:], codes01[:], early_scales[:])
+        multiply(acc2[:], codes2[:], scales2[:])
 
         last_pieces = [
-            hold.tile([P, end - begin, PACK], BF16, name=f"grouped3_{begin}", align_bytes=DMA_ALIGN)
+            hold.tile(
+                [P, end - begin, PACK], BF16, name=f"grouped3_{begin}",
+                tag="w_raw" if begin == 0 else f"grouped3_{begin}", align_bytes=DMA_ALIGN,
+            )
             for begin, end in LAST_CUTS
         ]
         for piece, (begin, end) in zip(last_pieces, LAST_CUTS):
@@ -130,6 +139,10 @@ def tile_attend_spmm_kernel(tc, wT, vT, offs, out):
             quantize_values(last_codes, last_scales, begin, piece[:])
         acc3 = psum.tile([NQ, P], F32, name="acc3")
         multiply(acc3[:], last_codes[:], last_scales[:])
-        staged_last = hold.tile([NQ, P], F32, name="staged_last", align_bytes=DMA_ALIGN)
-        nc.scalar.copy(out=staged_last[:], in_=acc3[:])
-        nc.sync.dma_start(out=result[:, LAST * P:], in_=staged_last[:])
+
+        staged = hold.tile([NQ, DV], F32, name="staged", align_bytes=DMA_ALIGN)
+        nc.scalar.copy(out=staged[:, :pair], in_=acc01[:])
+        nc.sync.dma_start(out=result[:, :pair], in_=staged[:, :pair])
+        nc.vector.tensor_copy(staged[:, pair:LAST * P], acc2[:])
+        nc.scalar.copy(out=staged[:, LAST * P:], in_=acc3[:])
+        nc.sync.dma_start(out=result[:, pair:], in_=staged[:, pair:])

@@ -43,22 +43,21 @@ def tile_attend_spmm_kernel(tc, wT, vT, offs, out):
         )
 
         offsets = hold.tile([P, N // LIST_ROWS], U16, name="offsets")
-        pools = [
-            hold.tile([P, T], F32, name=f"pool_v{b}", tag=f"pool{b}", align_bytes=DMA_ALIGN) for b in range(LAST)
-        ]
+        pools = [hold.tile([P, T], F32, name="pool2", align_bytes=DMA_ALIGN)]
         pools.append(placed.tile([P, T], F32, name="pool_last", offset=0, align_bytes=DMA_ALIGN))
-        windows = [tile[:] for tile in pools]
-        w_raw = hold.tile([P, PACK, NQ], F32, name="w_raw", tag="w_raw", align_bytes=DMA_ALIGN)
+        pool01 = hold.tile([P, PAIRED, T], F32, name="pool01", align_bytes=DMA_ALIGN)
+        windows = [pool01[:, b, :] for b in range(PAIRED)] + [tile[:] for tile in pools]
+        w_raw = placed.tile([P, PACK, NQ], F32, name="w_raw", offset=16384, align_bytes=DMA_ALIGN)
 
-        nc.sync.dma_start(out=windows[0], in_=vT[:P, :])
+        nc.sync.dma_start(out=pool01[:], in_=vT[:PAIRED * P, :].rearrange("(b p) t -> p b t", b=PAIRED))
         nc.sync.dma_start(offsets[:], offs)
-        for b in range(1, LAST):
+        for b in range(PAIRED, LAST):
             nc.sync.dma_start(out=windows[b], in_=vT[b * P:(b + 1) * P, :])
         nc.sync.dma_start(out=windows[LAST], in_=vT[LAST * P:, :])
         nc.sync.dma_start(out=w_raw[:], in_=wT.flatten_outer_dims().rearrange("(p t) q -> p t q", t=PACK))
 
-        codes01 = hold.tile([P, PAIRED * P], U32, name="codes01", tag=f"pool{PAIRED}", align_bytes=DMA_ALIGN)
-        codes2 = placed.tile([P, P], U32, name="codes2", offset=0, align_bytes=DMA_ALIGN)
+        codes01 = hold.tile([P, PAIRED * P], U32, name="codes01", align_bytes=DMA_ALIGN)
+        codes2 = hold.tile([P, P], U32, name="codes2", align_bytes=DMA_ALIGN)
         scales2 = hold.tile([P, P], U8, name="scales2", align_bytes=DMA_ALIGN)
         early_scales = hold.tile([P, PAIRED * P], U8, name="early_scales", align_bytes=DMA_ALIGN)
         last_codes = hold.tile([P, P], U32, name="last_codes", align_bytes=DMA_ALIGN)
@@ -66,11 +65,23 @@ def tile_attend_spmm_kernel(tc, wT, vT, offs, out):
         w_codes = hold.tile([P, NQ], U32, name="w_codes", align_bytes=DMA_ALIGN)
         w_scales = hold.tile([P, NQ], U8, name="w_scales", align_bytes=DMA_ALIGN)
 
+        def gather_alone_and_turn(b):
+            picked = hold.tile([P, 2, P, 2], BF16, name=f"picked{b}", align_bytes=DMA_ALIGN)
+            nc.vector.tensor_copy(picked[:].rearrange("d u p e -> d p u e"), windows[b].indirect(offsets[:]))
+            words = picked[:].rearrange("d u p e -> d (u p e)").bitcast(F32)
+            turned = psum.tile([P, 2, P], F32, name=f"turned{b}")
+            for u in range(2):
+                nc.tensor.transpose(turned[:, u, :], words[:, u * P:(u + 1) * P], ident[:])
+            return turned
+
         def gather_and_turn(b):
             picked = hold.tile([P, N], BF16, name=f"picked{b}", align_bytes=DMA_ALIGN)
-            cut = VECTOR_SLOTS // LIST_ROWS
-            nc.vector.tensor_copy(picked[:, :VECTOR_SLOTS], windows[b].indirect(offsets[:, :cut]))
-            nc.scalar.activation(picked[:, VECTOR_SLOTS:], windows[b].indirect(offsets[:, cut:]), COPY)
+            if b == LAST:
+                cut = VECTOR_SLOTS // LIST_ROWS
+                nc.vector.tensor_copy(picked[:, :VECTOR_SLOTS], windows[b].indirect(offsets[:, :cut]))
+                nc.scalar.activation(picked[:, VECTOR_SLOTS:], windows[b].indirect(offsets[:, cut:]), COPY)
+            else:
+                nc.scalar.activation(picked[:], windows[b].indirect(offsets[:]), COPY)
             words = picked[:].bitcast(F32)
             turned = psum.tile([P, 2, P], F32, name=f"turned{b}")
             for u in range(2):
@@ -99,11 +110,12 @@ def tile_attend_spmm_kernel(tc, wT, vT, offs, out):
                 stop=True,
             )
 
-        grouped = [hold.tile([P, P, PACK], BF16, name=f"grouped{b}", align_bytes=DMA_ALIGN) for b in range(LAST)]
-        for b in range(LAST):
-            group(grouped[b][:], gather_and_turn(b)[:])
+        turned = [gather_alone_and_turn(b) for b in range(PAIRED)]
+        turned2 = gather_and_turn(PAIRED)
         for b in range(PAIRED):
-            quantize_values(codes01, early_scales, b * P, grouped[b][:])
+            grouped = hold.tile([P, P, PACK], BF16, name=f"grouped{b}", align_bytes=DMA_ALIGN)
+            nc.vector.tensor_copy(grouped[:].bitcast(F32), turned[b][:].rearrange("p u r -> p r u"))
+            quantize_values(codes01, early_scales, b * P, grouped[:])
 
         turned_last = gather_and_turn(LAST)
 
@@ -112,24 +124,25 @@ def tile_attend_spmm_kernel(tc, wT, vT, offs, out):
         w_in = w_raw[:].rearrange("p t (c i) -> p c t i", i=LINE)
         nc.vector.tensor_copy(w_out[:, :20], w_in[:, :20])
         nc.scalar.copy(out=w_out[:, 20:], in_=w_in[:, 20:])
-        quantize_values(codes2, scales2, 0, grouped[PAIRED][:])
         nc.vector.quantize_mx(
             out=w_codes[:].bitcast(E5M2X4),
             scales=w_scales[:],
             in_=w_grouped[:].rearrange("p q t -> p (q t)"),
         )
 
-        result = out.flatten_outer_dims()
-        pair = PAIRED * P
-        acc01 = psum.tile([NQ, pair], F32, name="acc01")
-        acc2 = psum.tile([NQ, P], F32, name="acc2")
-        multiply(acc01[:], codes01[:], early_scales[:])
-        multiply(acc2[:], codes2[:], scales2[:])
+        grouped2 = placed.tile([P, P, PACK], BF16, name="grouped2", offset=16384, align_bytes=DMA_ALIGN)
+        group(grouped2[:], turned2[:])
+        quantize_values(codes2, scales2, 0, grouped2[:])
+
+        acc = [psum.tile([NQ, P], F32, name=f"acc{b}") for b in range(PARTS)]
+        for b in range(PAIRED):
+            multiply(acc[b][:], codes01[:, b * P:(b + 1) * P], early_scales[:, b * P:(b + 1) * P])
+        multiply(acc[PAIRED][:], codes2[:], scales2[:])
 
         last_pieces = [
-            hold.tile(
-                [P, end - begin, PACK], BF16, name=f"grouped3_{begin}",
-                tag="w_raw" if begin == 0 else f"grouped3_{begin}", align_bytes=DMA_ALIGN,
+            placed.tile(
+                [P, end - begin, PACK], BF16, name=f"grouped3_{begin}", offset=16384 + 1024 + 8 * begin,
+                align_bytes=DMA_ALIGN,
             )
             for begin, end in LAST_CUTS
         ]
@@ -137,12 +150,16 @@ def tile_attend_spmm_kernel(tc, wT, vT, offs, out):
             group(piece[:], turned_last[:, :, begin:end])
         for piece, (begin, end) in zip(last_pieces, LAST_CUTS):
             quantize_values(last_codes, last_scales, begin, piece[:])
-        acc3 = psum.tile([NQ, P], F32, name="acc3")
-        multiply(acc3[:], last_codes[:], last_scales[:])
+        multiply(acc[LAST][:], last_codes[:], last_scales[:])
 
+        result = out.flatten_outer_dims()
         staged = hold.tile([NQ, DV], F32, name="staged", align_bytes=DMA_ALIGN)
-        nc.scalar.copy(out=staged[:, :pair], in_=acc01[:])
-        nc.sync.dma_start(out=result[:, :pair], in_=staged[:, :pair])
-        nc.vector.tensor_copy(staged[:, pair:LAST * P], acc2[:])
-        nc.scalar.copy(out=staged[:, LAST * P:], in_=acc3[:])
-        nc.sync.dma_start(out=result[:, pair:], in_=staged[:, pair:])
+        for first, end in ((0, 2), (2, 3), (3, 4)):
+            for b in range(first, end):
+                cols = slice(b * P, (b + 1) * P)
+                if b % 2 == 0:
+                    nc.scalar.copy(out=staged[:, cols], in_=acc[b][:])
+                else:
+                    nc.vector.tensor_copy(staged[:, cols], acc[b][:])
+            cols = slice(first * P, end * P)
+            nc.sync.dma_start(out=result[:, cols], in_=staged[:, cols])

@@ -119,16 +119,19 @@ def tile_attend_spmm_kernel(tc, wT, vT, offs, out):
 
         turned_last = gather_and_turn(LAST)
 
-        w_grouped = placed.tile([P, NQ, PACK], BF16, name="w_grouped", offset=1024, align_bytes=DMA_ALIGN)
-        w_out = w_grouped[:].rearrange("p (c i) t -> p c t i", i=LINE)
-        w_in = w_raw[:].rearrange("p t (c i) -> p c t i", i=LINE)
-        nc.vector.tensor_copy(w_out[:, :20], w_in[:, :20])
-        nc.scalar.copy(out=w_out[:, 20:], in_=w_in[:, 20:])
-        nc.vector.quantize_mx(
-            out=w_codes[:].bitcast(E5M2X4),
-            scales=w_scales[:],
-            in_=w_grouped[:].rearrange("p q t -> p (q t)"),
-        )
+        half = NQ // 2
+        w_halves = [hold.tile([P, half, PACK], BF16, name=f"w_grouped{h}", align_bytes=DMA_ALIGN) for h in range(2)]
+        w_out = [tile[:].rearrange("p (c i) t -> p c t i", i=LINE) for tile in w_halves]
+        w_in = w_raw[:].rearrange("p t (h c i) -> p h c t i", h=2, i=LINE)
+        nc.scalar.copy(out=w_out[0], in_=w_in[:, 0])
+        nc.vector.tensor_copy(w_out[1], w_in[:, 1])
+        for h in range(2):
+            cols = slice(h * half, (h + 1) * half)
+            nc.vector.quantize_mx(
+                out=w_codes[:, cols].bitcast(E5M2X4),
+                scales=w_scales[:, cols],
+                in_=w_halves[h][:].rearrange("p q t -> p (q t)"),
+            )
 
         grouped2 = placed.tile([P, P, PACK], BF16, name="grouped2", offset=16384, align_bytes=DMA_ALIGN)
         group(grouped2[:], turned2[:])
@@ -153,13 +156,15 @@ def tile_attend_spmm_kernel(tc, wT, vT, offs, out):
         multiply(acc[LAST][:], last_codes[:], last_scales[:])
 
         result = out.flatten_outer_dims()
-        staged = hold.tile([NQ, DV], F32, name="staged", align_bytes=DMA_ALIGN)
         for first, end in ((0, 2), (2, 3), (3, 4)):
+            if first == 0:
+                staged = placed.tile([NQ, (end - first) * P], F32, name="staged0", offset=16384, align_bytes=DMA_ALIGN)
+            else:
+                staged = hold.tile([NQ, (end - first) * P], F32, name=f"staged{first}", align_bytes=DMA_ALIGN)
             for b in range(first, end):
-                cols = slice(b * P, (b + 1) * P)
-                if b % 2 == 0:
+                cols = slice((b - first) * P, (b - first + 1) * P)
+                if b in (1, 2):
                     nc.scalar.copy(out=staged[:, cols], in_=acc[b][:])
                 else:
                     nc.vector.tensor_copy(staged[:, cols], acc[b][:])
-            cols = slice(first * P, end * P)
-            nc.sync.dma_start(out=result[:, cols], in_=staged[:, cols])
+            nc.sync.dma_start(out=result[:, first * P:end * P], in_=staged[:])

@@ -1,6 +1,7 @@
 from contextlib import ExitStack
 
 import concourse.mybir as mybir
+from concourse.masks import make_identity
 
 N, T, DV, NQ = 512, 2048, 512, 128
 FLOPS = 2 * N * NQ * DV
@@ -13,7 +14,7 @@ LAST = PARTS - 1
 LINE = 4
 DMA_ALIGN = 256
 LIST_ROWS = 16
-VECTOR_SLOTS = 288
+VECTOR_SLOTS = 256
 LAST_CUTS = tuple((begin, begin + 32) for begin in range(0, P, 32))
 
 F32 = mybir.dt.float32
@@ -34,13 +35,7 @@ def tile_attend_spmm_kernel(tc, wT, vT, offs, out):
         psum = ctx.enter_context(tc.psum_pool(name="psum", bufs=1))
 
         ident = hold.tile([P, P], F32, name="ident", align_bytes=DMA_ALIGN)
-        zeros = hold.tile([P, P], F32, name="zeros", align_bytes=DMA_ALIGN)
-        nc.vector.memset(zeros[:], 0.0)
-        nc.scalar.copy(out=ident[:], in_=zeros[:])
-        nc.gpsimd.affine_select(
-            out=ident[:], in_=ident[:], compare_op=mybir.AluOpType.not_equal, fill=1.0, base=0,
-            pattern=[[-1, P]], channel_multiplier=1,
-        )
+        make_identity(nc, ident[:])
 
         offsets = hold.tile([P, N // LIST_ROWS], U16, name="offsets")
         pools = [hold.tile([P, T], F32, name="pool2", align_bytes=DMA_ALIGN)]
@@ -114,7 +109,10 @@ def tile_attend_spmm_kernel(tc, wT, vT, offs, out):
         turned2 = gather_and_turn(PAIRED)
         for b in range(PAIRED):
             grouped = hold.tile([P, P, PACK], BF16, name=f"grouped{b}", align_bytes=DMA_ALIGN)
-            nc.vector.tensor_copy(grouped[:].bitcast(F32), turned[b][:].rearrange("p u r -> p r u"))
+            if b == 0:
+                group(grouped[:], turned[b][:])
+            else:
+                nc.vector.tensor_copy(grouped[:].bitcast(F32), turned[b][:].rearrange("p u r -> p r u"))
             quantize_values(codes01, early_scales, b * P, grouped[:])
 
         turned_last = gather_and_turn(LAST)
@@ -156,14 +154,14 @@ def tile_attend_spmm_kernel(tc, wT, vT, offs, out):
         multiply(acc[LAST][:], last_codes[:], last_scales[:])
 
         result = out.flatten_outer_dims()
-        for first, end in ((0, 2), (2, 3), (3, 4)):
+        for first, end in ((0, 1), (1, 3), (3, 4)):
             if first == 0:
                 staged = placed.tile([NQ, (end - first) * P], F32, name="staged0", offset=16384, align_bytes=DMA_ALIGN)
             else:
                 staged = hold.tile([NQ, (end - first) * P], F32, name=f"staged{first}", align_bytes=DMA_ALIGN)
             for b in range(first, end):
                 cols = slice((b - first) * P, (b - first + 1) * P)
-                if b in (1, 2):
+                if b < PAIRED:
                     nc.scalar.copy(out=staged[:, cols], in_=acc[b][:])
                 else:
                     nc.vector.tensor_copy(staged[:, cols], acc[b][:])

@@ -9,13 +9,12 @@ FLOPS = 2 * N * NQ * DV
 P = 128
 PACK = 4
 PARTS = DV // P
-PAIRED = 2
 LAST = PARTS - 1
 LINE = 4
-DMA_ALIGN = 256
+ALIGN = 256
 LIST_ROWS = 16
-VECTOR_SLOTS = 256
-LAST_CUTS = tuple((begin, begin + 32) for begin in range(0, P, 32))
+SHARE = N // 2
+PIECE = 32
 
 F32 = mybir.dt.float32
 BF16 = mybir.dt.bfloat16
@@ -34,91 +33,85 @@ def tile_attend_spmm_kernel(tc, wT, vT, offs, out):
         placed = ctx.enter_context(tc.tile_pool(name="placed", bufs=1))
         psum = ctx.enter_context(tc.psum_pool(name="psum", bufs=1))
 
-        ident = hold.tile([P, P], F32, name="ident", align_bytes=DMA_ALIGN)
-        make_identity(nc, ident[:])
+        zeros = hold.tile([P, P], F32, name="zeros", align_bytes=ALIGN)
+        ident = hold.tile([P, P], F32, name="ident", align_bytes=ALIGN)
+        nc.vector.memset(zeros[:], 0.0)
+        nc.scalar.copy(out=ident[:], in_=zeros[:])
+        make_identity(nc, ident[:], nomemset=True)
 
         offsets = hold.tile([P, N // LIST_ROWS], U16, name="offsets")
-        pools = [hold.tile([P, T], F32, name="pool2", align_bytes=DMA_ALIGN)]
-        pools.append(placed.tile([P, T], F32, name="pool_last", offset=0, align_bytes=DMA_ALIGN))
-        pool01 = hold.tile([P, PAIRED, T], F32, name="pool01", align_bytes=DMA_ALIGN)
-        windows = [pool01[:, b, :] for b in range(PAIRED)] + [tile[:] for tile in pools]
-        w_raw = placed.tile([P, PACK, NQ], F32, name="w_raw", offset=16384, align_bytes=DMA_ALIGN)
+        pair = hold.tile([P, 2 * T], F32, name="pair", align_bytes=ALIGN)
+        pool2 = placed.tile([P, T], F32, name="pool2", offset=0, align_bytes=ALIGN)
+        pool3 = hold.tile([P, T], F32, name="pool3", align_bytes=ALIGN)
+        w_raw = placed.tile([P, PACK, NQ], F32, name="w_raw", offset=4 * T, align_bytes=ALIGN)
 
-        nc.sync.dma_start(out=pool01[:], in_=vT[:PAIRED * P, :].rearrange("(b p) t -> p b t", b=PAIRED))
+        nc.sync.dma_start(out=pair[:], in_=vT[:2 * P, :].rearrange("(p b) t -> p (b t)", b=2))
         nc.sync.dma_start(offsets[:], offs)
-        for b in range(PAIRED, LAST):
-            nc.sync.dma_start(out=windows[b], in_=vT[b * P:(b + 1) * P, :])
-        nc.sync.dma_start(out=windows[LAST], in_=vT[LAST * P:, :])
+        nc.sync.dma_start(out=pool2[:], in_=vT[2 * P:3 * P, :])
+        nc.sync.dma_start(out=pool3[:], in_=vT[3 * P:, :])
         nc.sync.dma_start(out=w_raw[:], in_=wT.flatten_outer_dims().rearrange("(p t) q -> p t q", t=PACK))
 
-        codes01 = hold.tile([P, PAIRED * P], U32, name="codes01", align_bytes=DMA_ALIGN)
-        codes2 = hold.tile([P, P], U32, name="codes2", align_bytes=DMA_ALIGN)
-        scales2 = hold.tile([P, P], U8, name="scales2", align_bytes=DMA_ALIGN)
-        early_scales = hold.tile([P, PAIRED * P], U8, name="early_scales", align_bytes=DMA_ALIGN)
-        last_codes = hold.tile([P, P], U32, name="last_codes", align_bytes=DMA_ALIGN)
-        last_scales = hold.tile([P, P], U8, name="last_scales", align_bytes=DMA_ALIGN)
-        w_codes = hold.tile([P, NQ], U32, name="w_codes", align_bytes=DMA_ALIGN)
-        w_scales = hold.tile([P, NQ], U8, name="w_scales", align_bytes=DMA_ALIGN)
+        pair_codes = hold.tile([P, 2 * P], U32, name="pair_codes", align_bytes=ALIGN)
+        pair_scales = hold.tile([P, 2 * P], U8, name="pair_scales", align_bytes=ALIGN)
+        codes = [pair_codes[:, :P], pair_codes[:, P:]]
+        scales = [pair_scales[:, :P], pair_scales[:, P:]]
+        codes.append(placed.tile([P, P], U32, name="codes2", offset=4 * T, align_bytes=ALIGN)[:])
+        codes.append(hold.tile([P, P], U32, name="codes3", align_bytes=ALIGN)[:])
+        scales.extend(hold.tile([P, P], U8, name=f"scales{b}", align_bytes=ALIGN)[:] for b in (2, 3))
+        w_codes = hold.tile([P, NQ], U32, name="w_codes", align_bytes=ALIGN)
+        w_scales = hold.tile([P, NQ], U8, name="w_scales", align_bytes=ALIGN)
+        pair_turned = psum.tile([P, 2, 2, P], F32, name="pair_turned")
+        turned = [pair_turned[:, 0], pair_turned[:, 1]]
+        turned.extend(psum.tile([P, 2, P], F32, name=f"turned{b}")[:] for b in (2, 3))
 
-        def gather_alone_and_turn(b):
-            picked = hold.tile([P, 2, P, 2], BF16, name=f"picked{b}", align_bytes=DMA_ALIGN)
-            nc.vector.tensor_copy(picked[:].rearrange("d u p e -> d p u e"), windows[b].indirect(offsets[:]))
-            words = picked[:].rearrange("d u p e -> d (u p e)").bitcast(F32)
-            turned = psum.tile([P, 2, P], F32, name=f"turned{b}")
-            for u in range(2):
-                nc.tensor.transpose(turned[:, u, :], words[:, u * P:(u + 1) * P], ident[:])
-            return turned
-
-        def gather_and_turn(b):
-            picked = hold.tile([P, N], BF16, name=f"picked{b}", align_bytes=DMA_ALIGN)
-            if b == LAST:
-                cut = VECTOR_SLOTS // LIST_ROWS
-                nc.vector.tensor_copy(picked[:, :VECTOR_SLOTS], windows[b].indirect(offsets[:, :cut]))
-                nc.scalar.activation(picked[:, VECTOR_SLOTS:], windows[b].indirect(offsets[:, cut:]), COPY)
-            else:
-                nc.scalar.activation(picked[:], windows[b].indirect(offsets[:]), COPY)
+        def turn_every_second_word(b, picked):
             words = picked[:].bitcast(F32)
-            turned = psum.tile([P, 2, P], F32, name=f"turned{b}")
             for u in range(2):
-                nc.tensor.transpose(turned[:, u, :], words[:, u::2], ident[:])
-            return turned
+                nc.tensor.transpose(turned[b][:, u, :], words[:, u::2], ident[:])
 
-        def group(grouped, turned):
-            nc.scalar.copy(out=grouped.bitcast(F32), in_=turned.rearrange("p u r -> p r u"))
+        def gather_shared(b, window):
+            picked = hold.tile([P, N], BF16, name=f"picked{b}", align_bytes=ALIGN)
+            cut = SHARE // LIST_ROWS
+            nc.vector.tensor_copy(picked[:, :SHARE], window[:].indirect(offsets[:, :cut]))
+            nc.scalar.activation(picked[:, SHARE:], window[:].indirect(offsets[:, cut:]), COPY)
+            turn_every_second_word(b, picked)
 
-        def quantize_values(codes, scales, first, grouped):
-            cols = slice(first, first + grouped.shape[1])
+        def interleaved(b, begin, end):
+            return turned[b][:, :, begin:end].rearrange("p u r -> p r u")
+
+        def quantize_values(b, begin, grouped):
+            cols = slice(begin, begin + grouped.shape[1])
             nc.vector.quantize_mx(
-                out=codes[:, cols].bitcast(E4M3X4),
-                scales=scales[:, cols],
-                in_=grouped.rearrange("p r t -> p (r t)"),
+                out=codes[b][:, cols].bitcast(E4M3X4),
+                scales=scales[b][:, cols],
+                in_=grouped[:].rearrange("p r t -> p (r t)"),
             )
 
-        def multiply(acc, codes, scales):
-            nc.tensor.matmul_mx(
-                out=acc,
-                lhsT=w_codes[:].bitcast(E5M2X4),
-                lhsT_scale=w_scales[:],
-                rhs=codes.bitcast(E4M3X4),
-                rhs_scale=scales,
-                start=True,
-                stop=True,
-            )
+        picked0 = hold.tile([P, N], BF16, name="picked0", align_bytes=ALIGN)
+        nc.scalar.activation(picked0[:], pair[:].indirect(offsets[:]), COPY)
+        picked1 = hold.tile([P, 2, P, 2], BF16, name="picked1", align_bytes=ALIGN)
+        nc.vector.tensor_copy(picked1[:].rearrange("d u p e -> d p u e"), pair[:, T:].indirect(offsets[:]))
+        turn_every_second_word(0, picked0)
+        words1 = picked1[:].rearrange("d u p e -> d (u p e)").bitcast(F32)
+        for u in range(2):
+            nc.tensor.transpose(turned[1][:, u, :], words1[:, u * P:(u + 1) * P], ident[:])
 
-        turned = [gather_alone_and_turn(b) for b in range(PAIRED)]
-        turned2 = gather_and_turn(PAIRED)
-        for b in range(PAIRED):
-            grouped = hold.tile([P, P, PACK], BF16, name=f"grouped{b}", align_bytes=DMA_ALIGN)
-            if b == 0:
-                group(grouped[:], turned[b][:])
-            else:
-                nc.vector.tensor_copy(grouped[:].bitcast(F32), turned[b][:].rearrange("p u r -> p r u"))
-            quantize_values(codes01, early_scales, b * P, grouped[:])
+        gather_shared(2, pool2)
 
-        turned_last = gather_and_turn(LAST)
+        pair_grouped = placed.tile([P, P, 2, PACK], BF16, name="pair_grouped", offset=0, align_bytes=ALIGN)
+        nc.vector.tensor_copy(pair_grouped[:].bitcast(F32), pair_turned[:].rearrange("p b u r -> p r b u"))
+        nc.vector.quantize_mx(
+            out=pair_codes[:].bitcast(E4M3X4),
+            scales=pair_scales[:],
+            in_=pair_grouped[:].rearrange("p r b t -> p (r b t)"),
+        )
+        grouped2 = hold.tile([P, P, PACK], BF16, name="grouped2", align_bytes=ALIGN)
+        nc.scalar.copy(out=grouped2[:].bitcast(F32), in_=interleaved(2, 0, P))
+
+        gather_shared(LAST, pool3)
 
         half = NQ // 2
-        w_halves = [hold.tile([P, half, PACK], BF16, name=f"w_grouped{h}", align_bytes=DMA_ALIGN) for h in range(2)]
+        w_halves = [hold.tile([P, half, PACK], BF16, name=f"w_grouped{h}", align_bytes=ALIGN) for h in range(2)]
         w_out = [tile[:].rearrange("p (c i) t -> p c t i", i=LINE) for tile in w_halves]
         w_in = w_raw[:].rearrange("p t (h c i) -> p h c t i", h=2, i=LINE)
         nc.scalar.copy(out=w_out[0], in_=w_in[:, 0])
@@ -131,37 +124,38 @@ def tile_attend_spmm_kernel(tc, wT, vT, offs, out):
                 in_=w_halves[h][:].rearrange("p q t -> p (q t)"),
             )
 
-        grouped2 = placed.tile([P, P, PACK], BF16, name="grouped2", offset=16384, align_bytes=DMA_ALIGN)
-        group(grouped2[:], turned2[:])
-        quantize_values(codes2, scales2, 0, grouped2[:])
+        quantize_values(2, 0, grouped2)
 
         acc = [psum.tile([NQ, P], F32, name=f"acc{b}") for b in range(PARTS)]
-        for b in range(PAIRED):
-            multiply(acc[b][:], codes01[:, b * P:(b + 1) * P], early_scales[:, b * P:(b + 1) * P])
-        multiply(acc[PAIRED][:], codes2[:], scales2[:])
 
-        last_pieces = [
-            placed.tile(
-                [P, end - begin, PACK], BF16, name=f"grouped3_{begin}", offset=16384 + 1024 + 8 * begin,
-                align_bytes=DMA_ALIGN,
+        def multiply(b):
+            nc.tensor.matmul_mx(
+                out=acc[b][:],
+                lhsT=w_codes[:].bitcast(E5M2X4),
+                lhsT_scale=w_scales[:],
+                rhs=codes[b].bitcast(E4M3X4),
+                rhs_scale=scales[b],
+                start=True,
+                stop=True,
             )
-            for begin, end in LAST_CUTS
-        ]
-        for piece, (begin, end) in zip(last_pieces, LAST_CUTS):
-            group(piece[:], turned_last[:, :, begin:end])
-        for piece, (begin, end) in zip(last_pieces, LAST_CUTS):
-            quantize_values(last_codes, last_scales, begin, piece[:])
-        multiply(acc[LAST][:], last_codes[:], last_scales[:])
+
+        for b in range(LAST):
+            multiply(b)
+
+        begins = range(0, P, PIECE)
+        pieces = [hold.tile([P, PIECE, PACK], BF16, name=f"piece{begin}", align_bytes=ALIGN) for begin in begins]
+        for piece, begin in zip(pieces, begins):
+            nc.scalar.copy(out=piece[:].bitcast(F32), in_=interleaved(LAST, begin, begin + PIECE))
+        for piece, begin in zip(pieces, begins):
+            quantize_values(LAST, begin, piece)
+        multiply(LAST)
 
         result = out.flatten_outer_dims()
         for first, end in ((0, 1), (1, 3), (3, 4)):
-            if first == 0:
-                staged = placed.tile([NQ, (end - first) * P], F32, name="staged0", offset=16384, align_bytes=DMA_ALIGN)
-            else:
-                staged = hold.tile([NQ, (end - first) * P], F32, name=f"staged{first}", align_bytes=DMA_ALIGN)
+            staged = hold.tile([NQ, (end - first) * P], F32, name=f"staged{first}", align_bytes=ALIGN)
             for b in range(first, end):
                 cols = slice((b - first) * P, (b - first + 1) * P)
-                if b < PAIRED:
+                if b < 2:
                     nc.scalar.copy(out=staged[:, cols], in_=acc[b][:])
                 else:
                     nc.vector.tensor_copy(staged[:, cols], acc[b][:])

@@ -15,6 +15,7 @@ ALIGN = 256
 LIST_ROWS = 16
 SHARE = N // 2
 PIECE = 32
+SCALAR_QUERIES = 32
 
 F32 = mybir.dt.float32
 BF16 = mybir.dt.bfloat16
@@ -112,10 +113,17 @@ def tile_attend_spmm_kernel(tc, wT, vT, offs, out):
 
         half = NQ // 2
         w_halves = [hold.tile([P, half, PACK], BF16, name=f"w_grouped{h}", align_bytes=ALIGN) for h in range(2)]
-        w_out = [tile[:].rearrange("p (c i) t -> p c t i", i=LINE) for tile in w_halves]
-        w_in = w_raw[:].rearrange("p t (h c i) -> p h c t i", h=2, i=LINE)
-        nc.scalar.copy(out=w_out[0], in_=w_in[:, 0])
-        nc.vector.tensor_copy(w_out[1], w_in[:, 1])
+
+        def round_weights(copy, begin, end):
+            h, first = divmod(begin, half)
+            copy(
+                w_halves[h][:, first:first + end - begin, :].rearrange("p (c i) t -> p c t i", i=LINE),
+                w_raw[:, :, begin:end].rearrange("p t (c i) -> p c t i", i=LINE),
+            )
+
+        round_weights(nc.vector.tensor_copy, 0, half)
+        round_weights(nc.vector.tensor_copy, half, NQ - SCALAR_QUERIES)
+        round_weights(nc.scalar.copy, NQ - SCALAR_QUERIES, NQ)
         for h in range(2):
             cols = slice(h * half, (h + 1) * half)
             nc.vector.quantize_mx(

@@ -56,9 +56,10 @@ def tile_attend_spmm_kernel(tc, wT, vT, offs, out):
         pair_scales = hold.tile([P, 2 * P], U8, name="pair_scales", align_bytes=ALIGN)
         codes = [pair_codes[:, :P], pair_codes[:, P:]]
         scales = [pair_scales[:, :P], pair_scales[:, P:]]
-        codes.append(placed.tile([P, P], U32, name="codes2", offset=4 * T, align_bytes=ALIGN)[:])
-        codes.append(hold.tile([P, P], U32, name="codes3", align_bytes=ALIGN)[:])
-        scales.extend(hold.tile([P, P], U8, name=f"scales{b}", align_bytes=ALIGN)[:] for b in (2, 3))
+        rest_codes = placed.tile([P, 2 * P], U32, name="rest_codes", offset=4 * T, align_bytes=ALIGN)
+        rest_scales = hold.tile([P, 2 * P], U8, name="rest_scales", align_bytes=ALIGN)
+        codes.extend([rest_codes[:, :P], rest_codes[:, P:]])
+        scales.extend([rest_scales[:, :P], rest_scales[:, P:]])
         w_codes = hold.tile([P, NQ], U32, name="w_codes", align_bytes=ALIGN)
         w_scales = hold.tile([P, NQ], U8, name="w_scales", align_bytes=ALIGN)
         pair_turned = psum.tile([P, 2, 2, P], F32, name="pair_turned")
@@ -134,21 +135,22 @@ def tile_attend_spmm_kernel(tc, wT, vT, offs, out):
 
         quantize_values(2, 0, grouped2)
 
-        acc = [psum.tile([NQ, P], F32, name=f"acc{b}") for b in range(PARTS)]
+        acc = [psum.tile([NQ, P], F32, name=f"acc{b}") for b in range(LAST)]
+        late = [psum.tile([NQ, P], F32, name=f"late{h}") for h in range(2)]
 
-        def multiply(b):
+        def multiply(bank, value_codes, value_scales):
             nc.tensor.matmul_mx(
-                out=acc[b][:],
+                out=bank[:],
                 lhsT=w_codes[:].bitcast(E5M2X4),
                 lhsT_scale=w_scales[:],
-                rhs=codes[b].bitcast(E4M3X4),
-                rhs_scale=scales[b],
+                rhs=value_codes.bitcast(E4M3X4),
+                rhs_scale=value_scales,
                 start=True,
                 stop=True,
             )
 
         for b in range(LAST):
-            multiply(b)
+            multiply(acc[b], codes[b], scales[b])
 
         begins = range(0, P, PIECE)
         pieces = [hold.tile([P, PIECE, PACK], BF16, name=f"piece{begin}", align_bytes=ALIGN) for begin in begins]
@@ -156,15 +158,17 @@ def tile_attend_spmm_kernel(tc, wT, vT, offs, out):
             nc.scalar.copy(out=piece[:].bitcast(F32), in_=interleaved(LAST, begin, begin + PIECE))
         for piece, begin in zip(pieces, begins):
             quantize_values(LAST, begin, piece)
-        multiply(LAST)
+        for h in range(2):
+            cols = slice((h + 1) * P // 2, (h + 3) * P // 2)
+            multiply(late[h], rest_codes[:, cols], rest_scales[:, cols])
 
         result = out.flatten_outer_dims()
-        for first, end in ((0, 1), (1, 3), (3, 4)):
-            staged = hold.tile([NQ, (end - first) * P], F32, name=f"staged{first}", align_bytes=ALIGN)
-            for b in range(first, end):
-                cols = slice((b - first) * P, (b - first + 1) * P)
-                if b < 2:
-                    nc.scalar.copy(out=staged[:, cols], in_=acc[b][:])
-                else:
-                    nc.vector.tensor_copy(staged[:, cols], acc[b][:])
-            nc.sync.dma_start(out=result[:, first * P:end * P], in_=staged[:])
+        staged = [hold.tile([NQ, n * P], F32, name=f"staged{k}", align_bytes=ALIGN) for k, n in enumerate((1, 2, 1))]
+        nc.scalar.copy(out=staged[0][:], in_=acc[0][:])
+        nc.sync.dma_start(out=result[:, :P], in_=staged[0][:])
+        nc.scalar.copy(out=staged[1][:, :P], in_=acc[1][:])
+        nc.vector.tensor_copy(staged[1][:, P:], acc[2][:])
+        nc.sync.dma_start(out=result[:, P:3 * P], in_=staged[1][:])
+        nc.scalar.copy(out=staged[2][:, :P // 2], in_=late[0][:, P // 2:])
+        nc.vector.tensor_copy(staged[2][:, P // 2:], late[1][:, P // 2:])
+        nc.sync.dma_start(out=result[:, 3 * P:], in_=staged[2][:])

@@ -167,8 +167,8 @@ def tile_attend_spmm_kernel(tc, wT, vT, offs, out):
         nc.scalar.copy(out=staged[0][:], in_=acc[0][:])
         nc.sync.dma_start(out=result[:, :P], in_=staged[0][:])
         nc.scalar.copy(out=staged[1][:, :P], in_=acc[1][:])
-        nc.vector.tensor_copy(staged[1][:, P:], acc[2][:])
+        nc.scalar.copy(out=staged[1][:, P:], in_=acc[2][:])
         nc.sync.dma_start(out=result[:, P:3 * P], in_=staged[1][:])
-        nc.scalar.copy(out=staged[2][:, :P // 2], in_=late[0][:, P // 2:])
+        nc.vector.tensor_copy(staged[2][:, :P // 2], late[0][:, P // 2:])
         nc.vector.tensor_copy(staged[2][:, P // 2:], late[1][:, P // 2:])
         nc.sync.dma_start(out=result[:, 3 * P:], in_=staged[2][:])

from contextlib import ExitStack

import concourse.mybir as mybir
from concourse.masks import make_identity

N, T, DV, NQ = 512, 2048, 512, 128
FLOPS = 2 * N * NQ * DV

P = 128
PACK = 4
PARTS = DV // P
LAST = PARTS - 1
LINE = 4
ALIGN = 256
LIST_ROWS = 16
SHARE = N // 2
PIECE = 32
SCALAR_QUERIES = 32

F32 = mybir.dt.float32
BF16 = mybir.dt.bfloat16
U32 = mybir.dt.uint32
U16 = mybir.dt.uint16
U8 = mybir.dt.uint8
E4M3X4 = mybir.dt.float8_e4m3fn_x4
E5M2X4 = mybir.dt.float8_e5m2_x4
COPY = mybir.ActivationFunctionType.Copy


def tile_attend_spmm_kernel(tc, wT, vT, offs, out):
    nc = tc.nc
    with ExitStack() as ctx:
        hold = ctx.enter_context(tc.tile_pool(name="hold", bufs=1))
        placed = ctx.enter_context(tc.tile_pool(name="placed", bufs=1))
        psum = ctx.enter_context(tc.psum_pool(name="psum", bufs=1))

        zeros = hold.tile([P, P], F32, name="zeros", align_bytes=ALIGN)
        ident = hold.tile([P, P], F32, name="ident", align_bytes=ALIGN)
        nc.vector.memset(zeros[:], 0.0)
        nc.scalar.copy(out=ident[:], in_=zeros[:])
        make_identity(nc, ident[:], nomemset=True)

        offsets = hold.tile([P, N // LIST_ROWS], U16, name="offsets")
        pair = hold.tile([P, 2 * T], F32, name="pair", align_bytes=ALIGN)
        pool2 = placed.tile([P, T], F32, name="pool2", offset=0, align_bytes=ALIGN)
        pool3 = hold.tile([P, T], F32, name="pool3", align_bytes=ALIGN)
        w_raw = placed.tile([P, PACK, NQ], F32, name="w_raw", offset=4 * T, align_bytes=ALIGN)

        nc.sync.dma_start(out=pair[:], in_=vT[:2 * P, :].rearrange("(p b) t -> p (b t)", b=2))
        nc.sync.dma_start(offsets[:], offs)
        nc.sync.dma_start(out=pool2[:], in_=vT[2 * P:3 * P, :])
        nc.sync.dma_start(out=pool3[:], in_=vT[3 * P:, :])
        nc.sync.dma_start(out=w_raw[:], in_=wT.flatten_outer_dims().rearrange("(p t) q -> p t q", t=PACK))

        pair_codes = hold.tile([P, 2 * P], U32, name="pair_codes", align_bytes=ALIGN)
        pair_scales = hold.tile([P, 2 * P], U8, name="pair_scales", align_bytes=ALIGN)
        codes = [pair_codes[:, :P], pair_codes[:, P:]]
        scales = [pair_scales[:, :P], pair_scales[:, P:]]
        rest_codes = placed.tile([P, 2 * P], U32, name="rest_codes", offset=4 * T, align_bytes=ALIGN)
        rest_scales = hold.tile([P, 2 * P], U8, name="rest_scales", align_bytes=ALIGN)
        codes.extend([rest_codes[:, :P], rest_codes[:, P:]])
        scales.extend([rest_scales[:, :P], rest_scales[:, P:]])
        w_codes = hold.tile([P, NQ], U32, name="w_codes", align_bytes=ALIGN)
        w_scales = hold.tile([P, NQ], U8, name="w_scales", align_bytes=ALIGN)
        pair_turned = psum.tile([P, 2, 2, P], F32, name="pair_turned")
        turned = [pair_turned[:, 0], pair_turned[:, 1]]
        turned.extend(psum.tile([P, 2, P], F32, name=f"turned{b}")[:] for b in (2, 3))

        def turn_every_second_word(b, picked):
            words = picked[:].bitcast(F32)
            for u in range(2):
                nc.tensor.transpose(turned[b][:, u, :], words[:, u::2], ident[:])

        def gather_shared(b, window):
            picked = hold.tile([P, N], BF16, name=f"picked{b}", align_bytes=ALIGN)
            cut = SHARE // LIST_ROWS
            nc.vector.tensor_copy(picked[:, :SHARE], window[:].indirect(offsets[:, :cut]))
            nc.scalar.activation(picked[:, SHARE:], window[:].indirect(offsets[:, cut:]), COPY)
            turn_every_second_word(b, picked)

        def interleaved(b, begin, end):
            return turned[b][:, :, begin:end].rearrange("p u r -> p r u")

        def quantize_values(b, begin, grouped):
            cols = slice(begin, begin + grouped.shape[1])
            nc.vector.quantize_mx(
                out=codes[b][:, cols].bitcast(E4M3X4),
                scales=scales[b][:, cols],
                in_=grouped[:].rearrange("p r t -> p (r t)"),
            )

        picked0 = hold.tile([P, N], BF16, name="picked0", align_bytes=ALIGN)
        nc.scalar.activation(picked0[:], pair[:].indirect(offsets[:]), COPY)
        picked1 = hold.tile([P, 2, P, 2], BF16, name="picked1", align_bytes=ALIGN)
        nc.vector.tensor_copy(picked1[:].rearrange("d u p e -> d p u e"), pair[:, T:].indirect(offsets[:]))
        turn_every_second_word(0, picked0)
        words1 = picked1[:].rearrange("d u p e -> d (u p e)").bitcast(F32)
        for u in range(2):
            nc.tensor.transpose(turned[1][:, u, :], words1[:, u * P:(u + 1) * P], ident[:])

        gather_shared(2, pool2)

        pair_grouped = placed.tile([P, P, 2, PACK], BF16, name="pair_grouped", offset=0, align_bytes=ALIGN)
        nc.vector.tensor_copy(pair_grouped[:].bitcast(F32), pair_turned[:].rearrange("p b u r -> p r b u"))
        nc.vector.quantize_mx(
            out=pair_codes[:].bitcast(E4M3X4),
            scales=pair_scales[:],
            in_=pair_grouped[:].rearrange("p r b t -> p (r b t)"),
        )
        grouped2 = hold.tile([P, P, PACK], BF16, name="grouped2", align_bytes=ALIGN)
        nc.scalar.copy(out=grouped2[:].bitcast(F32), in_=interleaved(2, 0, P))

        gather_shared(LAST, pool3)

        half = NQ // 2
        w_halves = [hold.tile([P, half, PACK], BF16, name=f"w_grouped{h}", align_bytes=ALIGN) for h in range(2)]

        def round_weights(copy, begin, end):
            h, first = divmod(begin, half)
            copy(
                w_halves[h][:, first:first + end - begin, :].rearrange("p (c i) t -> p c t i", i=LINE),
                w_raw[:, :, begin:end].rearrange("p t (c i) -> p c t i", i=LINE),
            )

        round_weights(nc.vector.tensor_copy, 0, half)
        round_weights(nc.vector.tensor_copy, half, NQ - SCALAR_QUERIES)
        round_weights(nc.scalar.copy, NQ - SCALAR_QUERIES, NQ)
        for h in range(2):
            cols = slice(h * half, (h + 1) * half)
            nc.vector.quantize_mx(
                out=w_codes[:, cols].bitcast(E5M2X4),
                scales=w_scales[:, cols],
                in_=w_halves[h][:].rearrange("p q t -> p (q t)"),
            )

        quantize_values(2, 0, grouped2)

        acc = [psum.tile([NQ, P], F32, name=f"acc{b}") for b in range(LAST)]
        late = [psum.tile([NQ, P], F32, name=f"late{h}") for h in range(2)]

        def multiply(bank, value_codes, value_scales):
            nc.tensor.matmul_mx(
                out=bank[:],
                lhsT=w_codes[:].bitcast(E5M2X4),
                lhsT_scale=w_scales[:],
                rhs=value_codes.bitcast(E4M3X4),
                rhs_scale=value_scales,
                start=True,
                stop=True,
            )

        for b in range(LAST):
            multiply(acc[b], codes[b], scales[b])

        begins = range(0, P, PIECE)
        pieces = [hold.tile([P, PIECE, PACK], BF16, name=f"piece{begin}", align_bytes=ALIGN) for begin in begins]
        for piece, begin in zip(pieces, begins):
            nc.scalar.copy(out=piece[:].bitcast(F32), in_=interleaved(LAST, begin, begin + PIECE))
        for piece, begin in zip(pieces, begins):
            quantize_values(LAST, begin, piece)
        for h in range(2):
            cols = slice((h + 1) * P // 2, (h + 3) * P // 2)
            multiply(late[h], rest_codes[:, cols], rest_scales[:, cols])

        result = out.flatten_outer_dims()
        staged = [hold.tile([NQ, n * P], F32, name=f"staged{k}", align_bytes=ALIGN) for k, n in enumerate((1, 2, 1))]
        nc.scalar.copy(out=staged[0][:], in_=acc[0][:])
        nc.sync.dma_start(out=result[:, :P], in_=staged[0][:])
        nc.scalar.copy(out=staged[1][:, :P], in_=acc[1][:])
        nc.scalar.copy(out=staged[1][:, P:], in_=acc[2][:])
        nc.sync.dma_start(out=result[:, P:3 * P], in_=staged[1][:])
        nc.vector.tensor_copy(staged[2][:, :P // 2], late[0][:, P // 2:])
        nc.vector.tensor_copy(staged[2][:, P // 2:], late[1][:, P // 2:])
        nc.sync.dma_start(out=result[:, 3 * P:], in_=staged[2][:])
